import numpy as np
import ml_dtypes


def mxq(x, axis, fmt="e4m3"):
    dtype, down = {"e4m3": (ml_dtypes.float8_e4m3fn, 7), "e5m2": (ml_dtypes.float8_e5m2, 14)}[fmt]
    v = np.moveaxis(np.asarray(x, np.float32).astype(ml_dtypes.bfloat16).astype(np.float64), axis, -1)
    blocks = v.reshape(v.shape[:-1] + (-1, 32))
    amax = np.abs(blocks).max(-1, keepdims=True)
    byte = np.maximum(np.where(amax > 0, np.frexp(amax)[1] - 1 + 127, 0) - down, 1)
    scale = np.exp2(byte - 127.0)
    codes = (blocks / scale).astype(np.float32).astype(dtype).astype(np.float64)
    return np.moveaxis((codes * scale).reshape(v.shape), -1, axis)


WIDE = False


def mx_kscale(k):
    if not WIDE:
        return np.ones(k)
    levels = np.array([10, -10, 5, -5, 0])
    if k % 512:
        return np.exp2(np.random.permutation(np.resize(levels, k // 32))).repeat(32)
    a = np.empty((k // 512, 16))
    for p in range(k // 512):
        a[p, :8] = np.random.permutation(np.resize(levels, 8))
        for g in range(8):
            far = levels[np.abs(levels - a[p, g]) >= 10]
            a[p, g + 8] = far[np.random.randint(len(far))]
    return np.exp2(a.ravel()).repeat(32)


def f64(x):
    return np.asarray(x).astype(np.float64)


def striped(idx):
    return np.tile(idx.reshape(-1, 16).T, (8, 1)).astype(np.uint16)


def unstriped(offs):
    return offs[:16].T.reshape(-1).astype(np.int64)


E2M1 = np.array([0.0, 0.5, 1.0, 1.5, 2.0, 3.0, 4.0, 6.0, -0.0, -0.5, -1.0, -1.5, -2.0, -3.0, -4.0, -6.0])


def pack_weight(w, fmt):
    k, n = w.shape
    w = f64(np.asarray(w, np.float32).astype(ml_dtypes.bfloat16)).reshape(k // 32, 32, n)
    amax = np.abs(w).max(1)
    if fmt == "e4m3":
        byte = np.frexp(amax)[1] - 1 + 127 - 7
    else:
        mant, ex = np.frexp(amax / 6.0)
        byte = np.where(mant > 0.5, ex, ex - 1) + 127
    byte = np.clip(np.where(amax > 0, byte, 1), 1, 254)
    scaled = (w * np.exp2(127.0 - byte)[:, None, :]).reshape(k, n).astype(np.float32)
    by_word = np.ascontiguousarray(scaled.reshape(k // 512, 128, 4, n).transpose(0, 1, 3, 2))
    if fmt == "e4m3":
        words = by_word.astype(ml_dtypes.float8_e4m3fn).view(np.uint8)
    else:
        c = by_word.astype(ml_dtypes.float4_e2m1fn).view(np.uint8) & 0xF
        words = (c[..., 0::2] | (c[..., 1::2] << 4)).reshape(k // 512, 128, 2 * n)
    return np.ascontiguousarray(words), np.ascontiguousarray(byte.astype(np.uint8).reshape(k // 512, 16, n))


def unpack_weight(words, scales, fmt):
    g, _, n = scales.shape
    words = np.ascontiguousarray(words).reshape(g, 128, n, -1)
    if fmt == "e4m3":
        vals = words.view(ml_dtypes.float8_e4m3fn).astype(np.float64)
    else:
        nib = np.empty((g, 128, n, 4), np.uint8)
        nib[..., 0::2] = words & 0xF
        nib[..., 1::2] = words >> 4
        vals = E2M1[nib]
    vals = vals * np.repeat(np.exp2(scales.astype(np.float64) - 127.0), 8, axis=1)[..., None]
    return vals.transpose(0, 1, 3, 2).reshape(g * 512, n)


def gelu(v):
    return 0.5 * v * (1.0 + np.tanh(np.sqrt(2.0 / np.pi) * (v + 0.044715 * v**3)))


def striped8(idx):
    return np.concatenate([v.reshape(-1, 16).T for v in idx]).astype(np.uint16)


def unstriped8(offs):
    return np.stack([offs[16 * g:16 * g + 16].T.reshape(-1) for g in range(8)]).astype(np.int64)


def heads(h, wgt, idx8):
    r = np.arange(h.shape[0])
    return wgt[r // 4 % 128] * h[r[:, None], idx8[r % 512 // 64]]


K, T, S, H, T2, P, N = 1536, 2048, 512, 1024, 1024, 512, 512

def setup_inputs():
    n = np.random.standard_normal
    s = mx_kscale(K)[:, None]
    u = mx_kscale(H)[:, None]
    tab_words, tab_scales = pack_weight(n((K, T)) * s, "e4m3")
    w4_words, w4_scales = pack_weight(0.55 * n((H, N)) / np.sqrt(H) / u, "e2m1")
    return {
        "tab_words": tab_words, "tab_scales": tab_scales,
        "offs": striped(np.random.permutation(T)[:S]),
        "w1": (0.53 * n((K, H)) / np.sqrt(K) / s).astype(np.float32),
        "gain": (2.0 * np.exp(0.3 * n(H)) * u[:, 0]).astype(np.float32),
        "page0": (n((H, T2)) * u).astype(np.float32),
        "wgs": np.exp(0.3 * n((128, S))).astype(np.float32),
        "offs2": striped(np.random.permutation(T2)[:S]),
        "wgt": np.repeat(np.random.uniform(0.5, 2.0, (8, P)), 16, axis=0).astype(np.float32),
        "offs3": striped8(np.stack([np.random.permutation(T2)[:P] for _ in range(8)])),
        "valve": np.exp(0.3 * n(H)).astype(np.float32),
        "w4_words": w4_words, "w4_scales": w4_scales,
        "w3": (0.7 * n((K, N)) / np.sqrt(K) / s).astype(np.float32),
        "bias": (0.4 * n(N)).astype(np.float32),
    }

def reference(tab_words, tab_scales, offs, w1, gain, page0, wgs, offs2, wgt, offs3, valve, w4_words, w4_scales, w3, bias):
    v = unpack_weight(tab_words, tab_scales, "e4m3")[:, unstriped(offs)]
    w4 = unpack_weight(w4_words, w4_scales, "e2m1")
    w1q = mxq(f64(w1), 0, "e4m3")
    w3q = mxq(f64(w3), 0, "e4m3")
    h = f64(gain)[:, None] * np.sin(w1q.T @ v)
    page = f64(page0).copy()
    page[:, unstriped(offs2)] = np.tile(f64(wgs), (H // 128, 1)) * h
    x = f64(valve)[:, None] * heads(page, f64(wgt), unstriped8(offs3))
    xq = mxq(x, 0, "e4m3")
    y = w4.T @ xq + w3q.T @ v
    return np.tanh(y + f64(bias)[:, None])

@@ -1,0 +1,331 @@
+import math
+from contextlib import ExitStack
+
+import concourse.mybir as mybir
+
+K, T, S, H, T2, N = 1536, 2048, 512, 1024, 1024, 512
+FLOPS = 2 * (K * H * S + H * N * S + K * N * S)
+
+F32 = mybir.dt.float32
+BF16 = mybir.dt.bfloat16
+I32 = mybir.dt.int32
+U32 = mybir.dt.uint32
+U16 = mybir.dt.uint16
+U8 = mybir.dt.uint8
+FP8X4 = mybir.dt.float8_e4m3fn_x4
+FP4X4 = mybir.dt.float4_e2m1fn_x4
+ACT = mybir.ActivationFunctionType
+ALU = mybir.AluOpType
+
+P = 128
+PACK = 4
+PASS = P * PACK
+K_PASSES = K // PASS
+H_PASSES = H // PASS
+N_TILES = N // P
+BANK = 512
+TWO_PI = 2.0 * math.pi
+ROUNDER = 1.5 * 2.0**23
+CHUNKS = ((0, 128), (128, 128), (256, 128), (384, 128))
+
+
+def tile_list_antiskid_valve_features_kernel(
+    tc, tab_words, tab_scales, offs, w1, gain, page0, wgs, offs2, wgt, offs3, valve, w4_words, w4_scales, w3, bias, out
+):
+    nc = tc.nc
+    with ExitStack() as ctx:
+        held = ctx.enter_context(tc.tile_pool(name="held", bufs=1))
+        ring = ctx.enter_context(tc.tile_pool(name="ring", bufs=2))
+        psum = ctx.enter_context(tc.psum_pool(name="psum", bufs=1))
+
+        tab_plane = held.tile([P, T], U8, name="tab_plane", align_bytes=64)
+        w4_plane = held.tile([P, H_PASSES, N], U8, name="w4_plane", align_bytes=64)
+        nc.vector.memset(tab_plane[:].bitcast(I32), 0)
+        nc.vector.memset(w4_plane[:].bitcast(I32), 0)
+        valve_t = held.tile([P, H_PASSES, PACK], F32, name="valve_t")
+        gain_t = held.tile([P, H_PASSES, PACK], F32, name="gain_t")
+        bias_t = held.tile([P, N_TILES], F32, name="bias_t")
+
+        list1 = held.tile([P, S // 16], U16, name="list1")
+        list2 = held.tile([P, S // 16], U16, name="list2")
+        list3 = held.tile([P, S // 16], U16, name="list3")
+
+        def load_rows(src):
+            raw = ring.tile([P, PACK, BANK], F32, name="raw", tag="raw", bufs=6)
+            nc.sync.dma_start(out=raw[:], in_=src.rearrange("(p j) c -> p j c", j=PACK))
+            return raw
+
+        def load_page(b, t):
+            page = held.tile([P, T2], F32, name="page%d%d" % (b, t))
+            rows = page0[PASS * b : PASS * (b + 1), :].rearrange("(p t) c -> p t c", t=PACK)
+            nc.sync.dma_start(out=page[:], in_=rows[:, t, :])
+            return page
+
+        def w1_rows(b, a):
+            return w1[PASS * a : PASS * (a + 1), PASS * b : PASS * (b + 1)]
+
+        w1_raw = {}
+        tab = []
+        wgt_t = held.tile([P, S], F32, name="wgt_t")
+        for a in range(K_PASSES):
+            w1_raw[0, a] = load_rows(w1_rows(0, a))
+            if a == 0:
+                nc.sync.dma_start(list1[:], offs)
+                nc.sync.dma_start(out=valve_t[:], in_=valve.rearrange("(b p t) -> p b t", b=H_PASSES, t=PACK))
+                nc.sync.dma_start(out=wgt_t[:], in_=wgt)
+                for q in range(4):
+                    nc.scalar.dma_start(
+                        out=tab_plane[32 * q : 32 * q + 4 * K_PASSES, :].bitcast(I32),
+                        in_=tab_scales[:, 4 * q : 4 * q + 4, :].bitcast(I32),
+                    )
+            words = held.tile([P, T], U32, name="tab%d" % a)
+            nc.sync.dma_start(out=words[:].bitcast(I32), in_=tab_words[a].rearrange("p t i -> p (t i)").bitcast(I32))
+            tab.append(words)
+        nc.sync.dma_start(list2[:], offs2)
+        nc.sync.dma_start(out=gain_t[:], in_=gain.rearrange("(b p t) -> p b t", b=H_PASSES, t=PACK))
+        wgs_t = held.tile([P, PACK, S], F32, name="wgs_t")
+        for q in (0, 2, 1, 3):
+            nc.sync.dma_start(out=wgs_t[32 * q : 32 * q + 32, :, :], in_=wgs.rearrange("(q t) s -> q t s", t=PACK))
+        pages = {}
+        pages[0, 0] = load_page(0, 0)
+        nc.sync.dma_start(list3[:], offs3)
+        pages[0, 1] = load_page(0, 1)
+        for a in range(K_PASSES):
+            w1_raw[1, a] = load_rows(w1_rows(1, a))
+        w3_raw = [load_rows(w3[PASS * a : PASS * (a + 1), :]) for a in range(K_PASSES - 1)]
+        pages[0, 2] = load_page(0, 2)
+        pages[0, 3] = load_page(0, 3)
+        w3_raw.append(load_rows(w3[PASS * (K_PASSES - 1) :, :]))
+        pages[1, 0] = load_page(1, 0)
+        pages[1, 1] = load_page(1, 1)
+        w4_t = held.tile([P, H_PASSES, 2 * N], U8, name="w4_t", align_bytes=64)
+        nc.sync.dma_start(out=w4_t[:].bitcast(I32), in_=w4_words.rearrange("a p c -> p a c").bitcast(I32))
+        pages[1, 2] = load_page(1, 2)
+        pages[1, 3] = load_page(1, 3)
+        for q in range(4):
+            nc.sync.dma_start(
+                out=w4_plane[32 * q : 32 * q + 4, :, :].bitcast(I32),
+                in_=w4_scales[:, 4 * q : 4 * q + 4, :].rearrange("a r c -> r a c").bitcast(I32),
+            )
+        with nc.allow_non_contiguous_dma(reason="one bias value for each partition"):
+            nc.sync.dma_start(out=bias_t[:], in_=bias.rearrange("(a p) -> p a", p=P))
+
+        def copy_on(engine):
+            return nc.vector.tensor_copy if engine == "vector" else nc.scalar.copy
+
+        stage = [held.tile([P, PACK * BANK], BF16, name="stage%d" % i, align_bytes=64) for i in range(4)]
+
+        def as_floats(ap, index):
+            return ap.bitcast(F32)[:, S * index : S * (index + 1)]
+
+        def weave_w1(rounded, raw, engine):
+            copy_on(engine)(
+                out=rounded.rearrange("p (t m j) -> p m j t", t=PACK, j=PACK),
+                in_=raw[:].rearrange("p j (m t) -> p m j t", t=PACK),
+            )
+            return rounded
+
+        def weave(rounded, raw, engine):
+            copy_on(engine)(
+                out=rounded.rearrange("p (c i j) -> p c j i", i=4, j=PACK),
+                in_=raw.rearrange("p j (c i) -> p c j i", i=4),
+            )
+            return rounded
+
+        def quantize(rounded, width, name):
+            codes = held.tile([P, width], U32, name=name + "_codes", align_bytes=64)
+            scales = held.tile([P, width], U8, name=name + "_scales", align_bytes=64)
+            nc.vector.quantize_mx(out=codes[:].bitcast(FP8X4), scales=scales[:], in_=rounded)
+            return codes, scales
+
+        def scaled(dst, src, factor):
+            nc.scalar.activation(out=dst, in_=src, func=ACT.Copy, scale=factor)
+            return dst
+
+        wgt_valve = {}
+        for b in range(H_PASSES):
+            for t in range(PACK):
+                dst = held.tile([P, S], F32, name="wgt_valve%d%d" % (b, t))
+                wgt_valve[b, t] = scaled(dst[:], wgt_t[:], valve_t[:, b, t : t + 1])
+
+        v_scales = held.tile([P, S], U8, name="v_scales", align_bytes=64)
+        v_codes = []
+        w1_q = {}
+        for a in range(K_PASSES):
+            w1_q[0, a] = quantize(weave_w1(stage[a][:], w1_raw[0, a], "vector"), BANK, "w1_0%d" % a)
+            if a == 0:
+                nc.vector.tensor_copy(v_scales[:], tab_plane[:].indirect(list1[:]))
+            picked = held.tile([P, S], U32, name="v_codes%d" % a, align_bytes=64)
+            nc.vector.tensor_copy(picked[:], tab[a][:].indirect(list1[:]))
+            v_codes.append(picked)
+
+        def first_product(b):
+            z = [psum.tile([P, S], F32, name="z%d" % t, tag="z%d" % t) for t in range(PACK)]
+            for a in range(K_PASSES):
+                codes, scales = w1_q[b, a]
+                for t in range(PACK):
+                    cols = slice(P * t, P * (t + 1))
+                    nc.tensor.matmul_mx(
+                        out=z[t][:],
+                        lhsT=codes[:, cols].bitcast(FP8X4),
+                        lhsT_scale=scales[:, cols],
+                        rhs=v_codes[a][:].bitcast(FP8X4),
+                        rhs_scale=v_scales[4 * a :, :],
+                        start=(a == 0),
+                        stop=(a == K_PASSES - 1),
+                    )
+            return z
+
+        turns = [held.tile([P, S], F32, name="turns%d" % t) for t in range(PACK)]
+        sine_tiles = [held.tile([P, S], F32, name="sine%d" % t) for t in range(PACK)]
+        sines = [sine_tiles[t][:] for t in range(PACK)]
+        frac_tiles = [held.tile([P, S], F32, name="frac%d" % t) for t in range(PACK)]
+        biased = [held.tile([P, S], U32, name="biased%d" % i) for i in range(2)]
+
+        def whole_turns(z, t):
+            turns_u = biased[t % 2]
+            nc.scalar.activation(out=turns_u[:], in_=z[t][:], func=ACT.Copy, scale=1.0 / TWO_PI, bias=ROUNDER)
+            nc.scalar.activation(out=turns[t][:], in_=turns_u[:], func=ACT.Copy, scale=1.0, bias=-ROUNDER)
+
+        def whole_turns_vector(z, t):
+            turns_i = biased[t % 2][:].bitcast(I32)
+            nc.vector.tensor_scalar(
+                out=turns_i, in0=z[t][:], scalar1=1.0 / TWO_PI, scalar2=ROUNDER, op0=ALU.mult, op1=ALU.add
+            )
+            nc.vector.tensor_scalar(out=turns[t][:], in0=turns_i, scalar1=-ROUNDER, scalar2=None, op0=ALU.add)
+
+        def reduce_angle(z, t):
+            frac = frac_tiles[t]
+            nc.vector.scalar_tensor_tensor(
+                out=frac[:], in0=z[t][:], scalar=1.0 / TWO_PI, in1=turns[t][:], op0=ALU.mult, op1=ALU.subtract
+            )
+            return frac
+
+        def sine(dst, frac):
+            nc.scalar.activation(out=dst, in_=frac[:], func=ACT.Sin, scale=TWO_PI)
+            return dst
+
+        def wgs_gain(b, t, dst=None, engine="scalar"):
+            if dst is None:
+                dst = held.tile([P, S], F32, name="wgs_gain%d%d" % (b, t))[:]
+            if engine == "scalar":
+                return scaled(dst, wgs_t[:, t, :], gain_t[:, b, t : t + 1])
+            nc.vector.tensor_scalar(out=dst, in0=wgs_t[:, t, :], scalar1=gain_t[:, b, t : t + 1], scalar2=None, op0=ALU.mult)
+            return dst
+
+        def scatter(b, t, sin_z, factor):
+            nc.vector.tensor_tensor(pages[b, t][:].indirect(list2[:]), sin_z, factor, ALU.mult)
+
+        def gather(dst, b, t, start, width):
+            offsets = list3[:, start // 16 : (start + width) // 16]
+            nc.vector.tensor_tensor(
+                dst, pages[b, t][:].indirect(offsets), wgt_valve[b, t][:, start : start + width], ALU.mult
+            )
+
+        z = first_product(0)
+        whole_turns_vector(z, 0)
+        for t in range(1, PACK):
+            whole_turns(z, t)
+        fracs = [reduce_angle(z, t) for t in range(PACK)]
+        factors = [wgs_gain(0, t, None, "vector") for t in range(2)]
+        for t in range(PACK):
+            sine(sines[t], fracs[t])
+        x0 = held.tile([P, PACK, S], F32, name="x0")
+        for t in range(2):
+            scatter(0, t, sines[t], factors[t])
+            gather(x0[:, t, :], 0, t, 0, S)
+        for a in range(K_PASSES):
+            w1_q[1, a] = quantize(weave_w1(stage[a][:], w1_raw[1, a], "scalar"), BANK, "w1_1%d" % a)
+        z = first_product(1)
+        scatter(0, 2, sines[2], wgs_gain(0, 2, as_floats(stage[2][:], 0), "vector"))
+        gather(x0[:, 2, :], 0, 2, 0, S)
+        scatter(0, 3, sines[3], wgs_gain(0, 3, frac_tiles[3][:]))
+        gather(x0[:, 3, :], 0, 3, 0, S)
+
+        w3_stage = (stage[3], stage[0], stage[1])
+
+        def quantize_w3(a):
+            return quantize(weave(w3_stage[a][:], w3_raw[a][:], "scalar"), BANK, "w3_%d" % a)
+
+        factors = [wgs_gain(1, t, w1_raw[1, K_PASSES - 1][:, t, :]) for t in range(PACK)]
+        w3_q = [quantize_w3(0)]
+        for t in range(PACK):
+            whole_turns(z, t)
+        fracs = [reduce_angle(z, t) for t in range(PACK)]
+        w3_q += [quantize_w3(a) for a in range(1, K_PASSES)]
+        sine(sines[0], fracs[0])
+        x0_q = quantize(weave(stage[3][:], x0[:], "scalar"), BANK, "x0")
+        for t in range(1, PACK):
+            sine(sines[t], fracs[t])
+        for t in range(PACK):
+            scatter(1, t, sines[t], factors[t])
+
+        banks = {}
+        for c, (start, width) in enumerate(CHUNKS):
+            per_bank = BANK // width
+            for g in range(N_TILES // per_bank):
+                bank = psum.tile([P, per_bank, width], F32, name="y%d%d" % (c, g))
+                for i in range(per_bank):
+                    banks[c, g * per_bank + i] = (bank, i, i == 0, i == per_bank - 1)
+
+        def output_pass(c, n, lhsT, lhsT_scale, rhs, rhs_scale, first, last):
+            bank, i, opens, closes = banks[c, n]
+            nc.tensor.matmul_mx(
+                out=bank[:, i, :],
+                lhsT=lhsT,
+                lhsT_scale=lhsT_scale,
+                rhs=rhs,
+                rhs_scale=rhs_scale,
+                start=first and opens,
+                stop=last and closes,
+            )
+
+        def w4_pass(c, b, codes, scales):
+            for n in range(N_TILES):
+                output_pass(
+                    c,
+                    n,
+                    w4_t[:, b, 2 * P * n : 2 * P * (n + 1)].bitcast(FP4X4),
+                    w4_plane[:, b, P * n : P * (n + 1)],
+                    codes.bitcast(FP8X4),
+                    scales,
+                    False,
+                    b == H_PASSES - 1,
+                )
+
+        for a in range(K_PASSES):
+            codes, scales = w3_q[a]
+            for c, (start, width) in enumerate(CHUNKS):
+                cols = slice(start, start + width)
+                for n in range(N_TILES):
+                    rows = slice(P * n, P * (n + 1))
+                    output_pass(
+                        c,
+                        n,
+                        codes[:, rows].bitcast(FP8X4),
+                        scales[:, rows],
+                        v_codes[a][:, cols].bitcast(FP8X4),
+                        v_scales[4 * a :, cols],
+                        a == 0,
+                        False,
+                    )
+        for c, (start, width) in enumerate(CHUNKS):
+            cols = slice(start, start + width)
+            w4_pass(c, 0, x0_q[0][:, cols], x0_q[1][:, cols])
+
+        x1_bytes = [sines[3], factors[3]] * 2
+        x1_rounded = [stage[c][:, :S] for c in range(len(CHUNKS))]
+        out_view = out.rearrange("(a p) m -> p a m", p=P)
+        for c, (start, width) in enumerate(CHUNKS):
+            last = c == len(CHUNKS) - 1
+            x1 = x1_bytes[c].rearrange("p (t c) -> p t c", t=PACK)
+            for t in range(PACK):
+                gather(x1[:, t, :], 1, t, start, width)
+            rounded = weave(x1_rounded[c], x1, "vector" if last else "scalar")
+            codes, scales = quantize(rounded, width, "x1_%d" % c)
+            w4_pass(c, 1, codes[:], scales[:])
+            result = ring.tile([P, N_TILES, width], F32, name="result", tag="raw", bufs=6)
+            for n in range(N_TILES):
+                bank, i = banks[c, n][:2]
+                nc.scalar.activation(out=result[:, n, :], in_=bank[:, i, :], func=ACT.Tanh, bias=bias_t[:, n : n + 1])
+            nc.sync.dma_start(out=out_view[:, :, start : start + width], in_=result[:])

@@ -2,6 +2,7 @@ import math
 from contextlib import ExitStack
 
 import concourse.mybir as mybir
+from concourse.masks import make_identity
 
 K, T, S, H, T2, N = 1536, 2048, 512, 1024, 1024, 512
 FLOPS = 2 * (K * H * S + H * N * S + K * N * S)
@@ -26,6 +27,7 @@ N_TILES = N // P
 BANK = 512
 TWO_PI = 2.0 * math.pi
 ROUNDER = 1.5 * 2.0**23
+HALVES = (slice(0, S // 2), slice(S // 2, S))
 CHUNKS = ((0, 128), (128, 128), (256, 128), (384, 128))
 
 
@@ -67,25 +69,30 @@ def tile_list_antiskid_valve_features_kernel(
         w1_raw = {}
         tab = []
         wgt_t = held.tile([P, S], F32, name="wgt_t")
-        for a in range(K_PASSES):
-            w1_raw[0, a] = load_rows(w1_rows(0, a))
-            if a == 0:
-                nc.sync.dma_start(list1[:], offs)
-                nc.sync.dma_start(out=valve_t[:], in_=valve.rearrange("(b p t) -> p b t", b=H_PASSES, t=PACK))
-                nc.sync.dma_start(out=wgt_t[:], in_=wgt)
-                for q in range(4):
-                    nc.scalar.dma_start(
-                        out=tab_plane[32 * q : 32 * q + 4 * K_PASSES, :].bitcast(I32),
-                        in_=tab_scales[:, 4 * q : 4 * q + 4, :].bitcast(I32),
-                    )
+        wgs_t = held.tile([P, S], F32, name="wgs_t")
+
+        def load_table(a):
             words = held.tile([P, T], U32, name="tab%d" % a)
             nc.sync.dma_start(out=words[:].bitcast(I32), in_=tab_words[a].rearrange("p t i -> p (t i)").bitcast(I32))
             tab.append(words)
-        nc.sync.dma_start(list2[:], offs2)
+
+        nc.sync.dma_start(out=wgs_t[:], in_=wgs)
+        w1_raw[0, 0] = load_rows(w1_rows(0, 0))
         nc.sync.dma_start(out=gain_t[:], in_=gain.rearrange("(b p t) -> p b t", b=H_PASSES, t=PACK))
-        wgs_t = held.tile([P, PACK, S], F32, name="wgs_t")
-        for q in (0, 2, 1, 3):
-            nc.sync.dma_start(out=wgs_t[32 * q : 32 * q + 32, :, :], in_=wgs.rearrange("(q t) s -> q t s", t=PACK))
+        load_table(0)
+        nc.sync.dma_start(list1[:], offs)
+        for q in range(4):
+            nc.sync.dma_start(
+                out=tab_plane[32 * q : 32 * q + 4 * K_PASSES, :].bitcast(I32),
+                in_=tab_scales[:, 4 * q : 4 * q + 4, :].bitcast(I32),
+            )
+        w1_raw[0, 1] = load_rows(w1_rows(0, 1))
+        nc.sync.dma_start(out=wgt_t[:], in_=wgt)
+        nc.sync.dma_start(out=valve_t[:], in_=valve.rearrange("(b p t) -> p b t", b=H_PASSES, t=PACK))
+        load_table(1)
+        w1_raw[0, 2] = load_rows(w1_rows(0, 2))
+        load_table(2)
+        nc.sync.dma_start(list2[:], offs2)
         pages = {}
         pages[0, 0] = load_page(0, 0)
         nc.sync.dma_start(list3[:], offs3)
@@ -115,6 +122,9 @@ def tile_list_antiskid_valve_features_kernel(
 
         stage = [held.tile([P, PACK * BANK], BF16, name="stage%d" % i, align_bytes=64) for i in range(4)]
 
+        def entries(offsets, cols):
+            return offsets[:, cols.start // 16 : cols.stop // 16]
+
         def as_floats(ap, index):
             return ap.bitcast(F32)[:, S * index : S * (index + 1)]
 
@@ -142,11 +152,37 @@ def tile_list_antiskid_valve_features_kernel(
             nc.scalar.activation(out=dst, in_=src, func=ACT.Copy, scale=factor)
             return dst
 
+        sums = [psum.tile([P, BANK], F32, name="sums%d" % t) for t in range(PACK)]
+        turned = [psum.tile([P, BANK], F32, name="turned%d" % t) for t in range(PACK)]
+        identity = held.tile([P, P], F32, name="identity")
+        make_identity(nc, identity[:])
+        x0 = held.tile([P, PACK, S], F32, name="x0", align_bytes=64)
+        warm = held.tile([P, 8], F32, name="warm")
+        nc.scalar.activation(out=warm[:, 0:1], in_=identity[:, 0:1], func=ACT.Silu)
+
+        def block(i):
+            return slice(P * i, P * (i + 1))
+
+        for jb in range(S // P):
+            nc.tensor.matmul(turned[3][:, block(jb)], wgs_t[:, block(jb)], identity[:], start=True, stop=True, is_transpose=True)
+        wgs_turned = x0[:].rearrange("p jb (t rep q) -> p jb t rep q", t=PACK, rep=4)
+        for rep in range(4):
+            nc.scalar.copy(out=wgs_turned[:, :, :, rep, :], in_=turned[3][:].rearrange("p (jb q t) -> p jb t q", t=PACK, jb=S // P))
+        wgs_gain = {}
+        for t in range(PACK):
+            for jb in range(S // P):
+                nc.tensor.matmul(turned[t][:, block(jb)], x0[:, jb, block(t)], identity[:], start=True, stop=True, is_transpose=True)
+            for b in range(H_PASSES):
+                dst = held.tile([P, S], F32, name="wgs_gain%d%d" % (b, t))
+                wgs_gain[b, t] = scaled(dst[:], turned[t][:], gain_t[:, b, t : t + 1])
+
         wgt_valve = {}
-        for b in range(H_PASSES):
+
+        def scale_wgt(b, dst):
             for t in range(PACK):
-                dst = held.tile([P, S], F32, name="wgt_valve%d%d" % (b, t))
-                wgt_valve[b, t] = scaled(dst[:], wgt_t[:], valve_t[:, b, t : t + 1])
+                wgt_valve[b, t] = scaled(dst[:, t, :], wgt_t[:], valve_t[:, b, t : t + 1])
+
+        scale_wgt(0, held.tile([P, PACK, S], F32, name="wgt_valve"))
 
         v_scales = held.tile([P, S], U8, name="v_scales", align_bytes=64)
         v_codes = []
@@ -156,65 +192,81 @@ def tile_list_antiskid_valve_features_kernel(
             if a == 0:
                 nc.vector.tensor_copy(v_scales[:], tab_plane[:].indirect(list1[:]))
             picked = held.tile([P, S], U32, name="v_codes%d" % a, align_bytes=64)
-            nc.vector.tensor_copy(picked[:], tab[a][:].indirect(list1[:]))
+            for cols in HALVES if a == K_PASSES - 1 else (slice(0, S),):
+                nc.vector.tensor_copy(picked[:, cols], tab[a][:].indirect(entries(list1, cols)))
             v_codes.append(picked)
 
-        def first_product(b):
-            z = [psum.tile([P, S], F32, name="z%d" % t, tag="z%d" % t) for t in range(PACK)]
+        def first_product(b, direct):
             for a in range(K_PASSES):
                 codes, scales = w1_q[b, a]
+                first, last = a == 0, a == K_PASSES - 1
                 for t in range(PACK):
-                    cols = slice(P * t, P * (t + 1))
-                    nc.tensor.matmul_mx(
-                        out=z[t][:],
-                        lhsT=codes[:, cols].bitcast(FP8X4),
-                        lhsT_scale=scales[:, cols],
-                        rhs=v_codes[a][:].bitcast(FP8X4),
-                        rhs_scale=v_scales[4 * a :, :],
-                        start=(a == 0),
-                        stop=(a == K_PASSES - 1),
-                    )
-            return z
+                    if t in direct:
+                        for bank, cols in zip((sums[t], turned[t]), HALVES):
+                            nc.tensor.matmul_mx(
+                                out=bank[:, cols],
+                                lhsT=codes[:, block(t)].bitcast(FP8X4),
+                                lhsT_scale=scales[:, block(t)],
+                                rhs=v_codes[a][:, cols].bitcast(FP8X4),
+                                rhs_scale=v_scales[4 * a :, cols],
+                                start=first,
+                                stop=last,
+                            )
+                        continue
+                    for jb in range(S // P):
+                        nc.tensor.matmul_mx(
+                            out=sums[t][:, block(jb)],
+                            lhsT=v_codes[a][:, block(jb)].bitcast(FP8X4),
+                            lhsT_scale=v_scales[4 * a :, block(jb)],
+                            rhs=codes[:, block(t)].bitcast(FP8X4),
+                            rhs_scale=scales[:, block(t)],
+                            start=first and jb == 0,
+                            stop=last and jb == S // P - 1,
+                        )
 
-        turns = [held.tile([P, S], F32, name="turns%d" % t) for t in range(PACK)]
-        sine_tiles = [held.tile([P, S], F32, name="sine%d" % t) for t in range(PACK)]
-        sines = [sine_tiles[t][:] for t in range(PACK)]
-        frac_tiles = [held.tile([P, S], F32, name="frac%d" % t) for t in range(PACK)]
-        biased = [held.tile([P, S], U32, name="biased%d" % i) for i in range(2)]
+        sine_tiles = [held.tile([P, S], F32, name="sine%d" % t) for t in range(PACK - 1)]
+        sines = [tile[:] for tile in sine_tiles]
 
-        def whole_turns(z, t):
-            turns_u = biased[t % 2]
-            nc.scalar.activation(out=turns_u[:], in_=z[t][:], func=ACT.Copy, scale=1.0 / TWO_PI, bias=ROUNDER)
-            nc.scalar.activation(out=turns[t][:], in_=turns_u[:], func=ACT.Copy, scale=1.0, bias=-ROUNDER)
+        terms = held.tile([P, PACK, S], F32, name="terms")
+        biased_first = held.tile([P, S], I32, name="biased_first")
 
-        def whole_turns_vector(z, t):
-            turns_i = biased[t % 2][:].bitcast(I32)
+        def reduce_on_vector(z, cols):
+            frac, whole = as_floats(stage[0][:], 0)[:, cols], as_floats(stage[0][:], 1)[:, cols]
+            biased = biased_first[:, cols]
             nc.vector.tensor_scalar(
-                out=turns_i, in0=z[t][:], scalar1=1.0 / TWO_PI, scalar2=ROUNDER, op0=ALU.mult, op1=ALU.add
+                out=biased, in0=z, scalar1=1.0 / TWO_PI, scalar2=ROUNDER, op0=ALU.mult, op1=ALU.add
             )
-            nc.vector.tensor_scalar(out=turns[t][:], in0=turns_i, scalar1=-ROUNDER, scalar2=None, op0=ALU.add)
-
-        def reduce_angle(z, t):
-            frac = frac_tiles[t]
+            nc.vector.tensor_scalar(out=whole, in0=biased, scalar1=-ROUNDER, scalar2=None, op0=ALU.add)
             nc.vector.scalar_tensor_tensor(
-                out=frac[:], in0=z[t][:], scalar=1.0 / TWO_PI, in1=turns[t][:], op0=ALU.mult, op1=ALU.subtract
+                out=frac, in0=z, scalar=1.0 / TWO_PI, in1=whole, op0=ALU.mult, op1=ALU.subtract
             )
             return frac
 
+        def reduce_on_tensor(t, turns, minus_whole):
+            biased = ring.tile([P, S], U32, name="biased", tag="biased")
+            nc.scalar.activation(out=turns, in_=sums[t][:], func=ACT.Copy, scale=1.0 / TWO_PI)
+            nc.scalar.activation(out=biased[:], in_=turns, func=ACT.Copy, scale=1.0, bias=ROUNDER)
+            nc.scalar.activation(out=minus_whole, in_=biased[:], func=ACT.Copy, scale=-1.0, bias=ROUNDER)
+            for i, term in enumerate((turns, minus_whole)):
+                for jb in range(S // P):
+                    nc.tensor.matmul(
+                        turned[t][:, block(jb)],
+                        term[:, block(jb)],
+                        identity[:],
+                        start=(i == 0 and jb == 0),
+                        stop=(i == 1 and jb == S // P - 1),
+                        is_transpose=True,
+                    )
+            return turned[t][:]
+
         def sine(dst, frac):
-            nc.scalar.activation(out=dst, in_=frac[:], func=ACT.Sin, scale=TWO_PI)
+            nc.scalar.activation(out=dst, in_=frac, func=ACT.Sin, scale=TWO_PI)
             return dst
 
-        def wgs_gain(b, t, dst=None, engine="scalar"):
-            if dst is None:
-                dst = held.tile([P, S], F32, name="wgs_gain%d%d" % (b, t))[:]
-            if engine == "scalar":
-                return scaled(dst, wgs_t[:, t, :], gain_t[:, b, t : t + 1])
-            nc.vector.tensor_scalar(out=dst, in0=wgs_t[:, t, :], scalar1=gain_t[:, b, t : t + 1], scalar2=None, op0=ALU.mult)
-            return dst
-
-        def scatter(b, t, sin_z, factor):
-            nc.vector.tensor_tensor(pages[b, t][:].indirect(list2[:]), sin_z, factor, ALU.mult)
+        def scatter(b, t, sin_z, cols=slice(0, S)):
+            nc.vector.tensor_tensor(
+                pages[b, t][:].indirect(entries(list2, cols)), sin_z, wgs_gain[b, t][:, cols], ALU.mult
+            )
 
         def gather(dst, b, t, start, width):
             offsets = list3[:, start // 16 : (start + width) // 16]
@@ -222,49 +274,54 @@ def tile_list_antiskid_valve_features_kernel(
                 dst, pages[b, t][:].indirect(offsets), wgt_valve[b, t][:, start : start + width], ALU.mult
             )
 
-        z = first_product(0)
-        whole_turns_vector(z, 0)
-        for t in range(1, PACK):
-            whole_turns(z, t)
-        fracs = [reduce_angle(z, t) for t in range(PACK)]
-        factors = [wgs_gain(0, t, None, "vector") for t in range(2)]
-        for t in range(PACK):
-            sine(sines[t], fracs[t])
-        x0 = held.tile([P, PACK, S], F32, name="x0")
+        first_product(0, (0,))
+        first_fracs = [reduce_on_vector(bank[:, cols], cols) for bank, cols in zip((sums[0], turned[0]), HALVES)]
+        for frac, cols in zip(first_fracs, HALVES):
+            scatter(0, 0, sine(as_floats(stage[1][:], 0)[:, cols], frac), cols)
+        scatter(0, 1, sine(sines[1], reduce_on_tensor(1, terms[:, 0, :], terms[:, 1, :])))
+        w1_stage = (stage[0][:], x0[:, 1:3, :].rearrange("p t c -> p (t c)").bitcast(BF16), stage[2][:])
+
+        def quantize_w1(a):
+            w1_q[1, a] = quantize(weave_w1(w1_stage[a], w1_raw[1, a], "scalar"), BANK, "w1_1%d" % a)
+
+        quantize_w1(0)
+        scatter(0, 2, sine(sines[2], reduce_on_tensor(2, terms[:, 2, :], terms[:, 3, :])))
+        quantize_w1(1)
         for t in range(2):
-            scatter(0, t, sines[t], factors[t])
             gather(x0[:, t, :], 0, t, 0, S)
-        for a in range(K_PASSES):
-            w1_q[1, a] = quantize(weave_w1(stage[a][:], w1_raw[1, a], "scalar"), BANK, "w1_1%d" % a)
-        z = first_product(1)
-        scatter(0, 2, sines[2], wgs_gain(0, 2, as_floats(stage[2][:], 0), "vector"))
-        gather(x0[:, 2, :], 0, 2, 0, S)
-        scatter(0, 3, sines[3], wgs_gain(0, 3, frac_tiles[3][:]))
-        gather(x0[:, 3, :], 0, 3, 0, S)
+        quantize_w1(2)
+        last_terms = [as_floats(stage[3][:], h) for h in range(2)]
+        scatter(0, 3, sine(terms[:, 0, :], reduce_on_tensor(3, *last_terms)))
+        fracs = {}
+        second_terms = [[terms[:, 2 + h, :] for h in range(2)]]
+        second_terms.append([as_floats(stage[0][:], h) for h in range(2)])
+        second_terms.append([as_floats(stage[i][:], 0) for i in (1, 2)])
+        second_terms.append([terms[:, h, :] for h in range(2)])
+        first_product(1, ())
 
         w3_stage = (stage[3], stage[0], stage[1])
 
         def quantize_w3(a):
             return quantize(weave(w3_stage[a][:], w3_raw[a][:], "scalar"), BANK, "w3_%d" % a)
 
-        factors = [wgs_gain(1, t, w1_raw[1, K_PASSES - 1][:, t, :]) for t in range(PACK)]
         w3_q = [quantize_w3(0)]
+        for t in range(2, PACK):
+            gather(x0[:, t, :], 0, t, 0, S)
         for t in range(PACK):
-            whole_turns(z, t)
-        fracs = [reduce_angle(z, t) for t in range(PACK)]
+            fracs[t] = reduce_on_tensor(t, *second_terms[t])
+            if t < PACK - 1:
+                scatter(1, t, sine(sines[t], fracs[t]))
         w3_q += [quantize_w3(a) for a in range(1, K_PASSES)]
-        sine(sines[0], fracs[0])
-        x0_q = quantize(weave(stage[3][:], x0[:], "scalar"), BANK, "x0")
-        for t in range(1, PACK):
-            sine(sines[t], fracs[t])
-        for t in range(PACK):
-            scatter(1, t, sines[t], factors[t])
+        x0_q = quantize(weave(stage[2][:], x0[:], "scalar"), BANK, "x0")
+        last_sine = sine(x0[:, 0, :], fracs[PACK - 1])
+        scale_wgt(1, w3_raw[K_PASSES - 1])
+        scatter(1, PACK - 1, last_sine)
 
         banks = {}
         for c, (start, width) in enumerate(CHUNKS):
             per_bank = BANK // width
             for g in range(N_TILES // per_bank):
-                bank = psum.tile([P, per_bank, width], F32, name="y%d%d" % (c, g))
+                bank = turned[c][:].rearrange("p (i c) -> p i c", i=per_bank)
                 for i in range(per_bank):
                     banks[c, g * per_bank + i] = (bank, i, i == 0, i == per_bank - 1)
 
@@ -313,17 +370,17 @@ def tile_list_antiskid_valve_features_kernel(
             cols = slice(start, start + width)
             w4_pass(c, 0, x0_q[0][:, cols], x0_q[1][:, cols])
 
-        x1_bytes = [sines[3], factors[3]] * 2
+        x1_bytes = [last_sine, wgs_gain[1, 3]] * 2
         x1_rounded = [stage[c][:, :S] for c in range(len(CHUNKS))]
         out_view = out.rearrange("(a p) m -> p a m", p=P)
         for c, (start, width) in enumerate(CHUNKS):
-            last = c == len(CHUNKS) - 1
             x1 = x1_bytes[c].rearrange("p (t c) -> p t c", t=PACK)
             for t in range(PACK):
                 gather(x1[:, t, :], 1, t, start, width)
-            rounded = weave(x1_rounded[c], x1, "vector" if last else "scalar")
+            rounded = weave(x1_rounded[c], x1, "vector" if c >= 2 else "scalar")
             codes, scales = quantize(rounded, width, "x1_%d" % c)
             w4_pass(c, 1, codes[:], scales[:])
+        for c, (start, width) in enumerate(CHUNKS):
             result = ring.tile([P, N_TILES, width], F32, name="result", tag="raw", bufs=6)
             for n in range(N_TILES):
                 bank, i = banks[c, n][:2]

@@ -128,11 +128,14 @@ def tile_list_antiskid_valve_features_kernel(
         def as_floats(ap, index):
             return ap.bitcast(F32)[:, S * index : S * (index + 1)]
 
-        def weave_w1(rounded, raw, engine):
-            copy_on(engine)(
-                out=rounded.rearrange("p (t m j) -> p m j t", t=PACK, j=PACK),
-                in_=raw[:].rearrange("p j (m t) -> p m j t", t=PACK),
-            )
+        def weave_w1(rounded, raw, engines):
+            share = PACK // len(engines)
+            for i, engine in enumerate(engines):
+                part = slice(share * i, share * (i + 1))
+                copy_on(engine)(
+                    out=rounded.rearrange("p (t m j) -> p m j t", t=PACK, j=PACK)[:, :, :, part],
+                    in_=raw[:].rearrange("p j (m t) -> p m j t", t=PACK)[:, :, :, part],
+                )
             return rounded
 
         def weave(rounded, raw, engine):
@@ -164,17 +167,17 @@ def tile_list_antiskid_valve_features_kernel(
             return slice(P * i, P * (i + 1))
 
         for jb in range(S // P):
-            nc.tensor.matmul(turned[3][:, block(jb)], wgs_t[:, block(jb)], identity[:], start=True, stop=True, is_transpose=True)
+            nc.tensor.matmul(turned[0][:, block(jb)], wgs_t[:, block(jb)], identity[:], start=True, stop=True, is_transpose=True)
         wgs_turned = x0[:].rearrange("p jb (t rep q) -> p jb t rep q", t=PACK, rep=4)
         for rep in range(4):
-            nc.scalar.copy(out=wgs_turned[:, :, :, rep, :], in_=turned[3][:].rearrange("p (jb q t) -> p jb t q", t=PACK, jb=S // P))
+            nc.scalar.copy(out=wgs_turned[:, :, :, rep, :], in_=turned[0][:].rearrange("p (jb q t) -> p jb t q", t=PACK, jb=S // P))
         wgs_gain = {}
         for t in range(PACK):
             for jb in range(S // P):
-                nc.tensor.matmul(turned[t][:, block(jb)], x0[:, jb, block(t)], identity[:], start=True, stop=True, is_transpose=True)
+                nc.tensor.matmul(sums[t][:, block(jb)], x0[:, jb, block(t)], identity[:], start=True, stop=True, is_transpose=True)
             for b in range(H_PASSES):
                 dst = held.tile([P, S], F32, name="wgs_gain%d%d" % (b, t))
-                wgs_gain[b, t] = scaled(dst[:], turned[t][:], gain_t[:, b, t : t + 1])
+                wgs_gain[b, t] = scaled(dst[:], sums[t][:], gain_t[:, b, t : t + 1])
 
         wgt_valve = {}
 
@@ -182,13 +185,14 @@ def tile_list_antiskid_valve_features_kernel(
             for t in range(PACK):
                 wgt_valve[b, t] = scaled(dst[:, t, :], wgt_t[:], valve_t[:, b, t : t + 1])
 
-        scale_wgt(0, held.tile([P, PACK, S], F32, name="wgt_valve"))
+        for b in range(H_PASSES):
+            scale_wgt(b, held.tile([P, PACK, S], F32, name="wgt_valve%d" % b))
 
         v_scales = held.tile([P, S], U8, name="v_scales", align_bytes=64)
         v_codes = []
         w1_q = {}
         for a in range(K_PASSES):
-            w1_q[0, a] = quantize(weave_w1(stage[a][:], w1_raw[0, a], "vector"), BANK, "w1_0%d" % a)
+            w1_q[0, a] = quantize(weave_w1(stage[a][:], w1_raw[0, a], ("vector",)), BANK, "w1_0%d" % a)
             if a == 0:
                 nc.vector.tensor_copy(v_scales[:], tab_plane[:].indirect(list1[:]))
             picked = held.tile([P, S], U32, name="v_codes%d" % a, align_bytes=64)
@@ -224,10 +228,10 @@ def tile_list_antiskid_valve_features_kernel(
                             stop=last and jb == S // P - 1,
                         )
 
-        sine_tiles = [held.tile([P, S], F32, name="sine%d" % t) for t in range(PACK - 1)]
+        sine_tiles = [held.tile([P, S], F32, name="sine%d" % t) for t in range(PACK)]
         sines = [tile[:] for tile in sine_tiles]
 
-        terms = held.tile([P, PACK, S], F32, name="terms")
+        terms = held.tile([P, 3, S], F32, name="terms")
         biased_first = held.tile([P, S], I32, name="biased_first")
 
         def reduce_on_vector(z, cols):
@@ -278,26 +282,21 @@ def tile_list_antiskid_valve_features_kernel(
         first_fracs = [reduce_on_vector(bank[:, cols], cols) for bank, cols in zip((sums[0], turned[0]), HALVES)]
         for frac, cols in zip(first_fracs, HALVES):
             scatter(0, 0, sine(as_floats(stage[1][:], 0)[:, cols], frac), cols)
-        scatter(0, 1, sine(sines[1], reduce_on_tensor(1, terms[:, 0, :], terms[:, 1, :])))
-        w1_stage = (stage[0][:], x0[:, 1:3, :].rearrange("p t c -> p (t c)").bitcast(BF16), stage[2][:])
-
-        def quantize_w1(a):
-            w1_q[1, a] = quantize(weave_w1(w1_stage[a], w1_raw[1, a], "scalar"), BANK, "w1_1%d" % a)
-
-        quantize_w1(0)
-        scatter(0, 2, sine(sines[2], reduce_on_tensor(2, terms[:, 2, :], terms[:, 3, :])))
-        quantize_w1(1)
-        for t in range(2):
-            gather(x0[:, t, :], 0, t, 0, S)
-        quantize_w1(2)
-        last_terms = [as_floats(stage[3][:], h) for h in range(2)]
-        scatter(0, 3, sine(terms[:, 0, :], reduce_on_tensor(3, *last_terms)))
-        fracs = {}
-        second_terms = [[terms[:, 2 + h, :] for h in range(2)]]
-        second_terms.append([as_floats(stage[0][:], h) for h in range(2)])
-        second_terms.append([as_floats(stage[i][:], 0) for i in (1, 2)])
-        second_terms.append([terms[:, h, :] for h in range(2)])
+        first_terms = {
+            1: (terms[:, 0, :], terms[:, 1, :]),
+            2: (terms[:, 2, :], as_floats(stage[0][:], 1)),
+            3: (as_floats(stage[2][:], 0), x0[:, 2, :]),
+        }
+        for t in range(1, PACK - 1):
+            scatter(0, t, sine(sines[t], reduce_on_tensor(t, *first_terms[t])))
+        last_frac = reduce_on_tensor(PACK - 1, *first_terms[PACK - 1])
+        w1_stage = (stage[0][:], stage[2][:], x0[:, 2:4, :].rearrange("p t c -> p (t c)").bitcast(BF16))
+        for a in range(K_PASSES):
+            w1_q[1, a] = quantize(weave_w1(w1_stage[a], w1_raw[1, a], ("scalar",)), BANK, "w1_1%d" % a)
+        scatter(0, PACK - 1, sine(w1_raw[1, K_PASSES - 1][:, 0, :], last_frac))
         first_product(1, ())
+        for t in range(PACK):
+            gather(x0[:, t, :], 0, t, 0, S)
 
         w3_stage = (stage[3], stage[0], stage[1])
 
@@ -305,17 +304,11 @@ def tile_list_antiskid_valve_features_kernel(
             return quantize(weave(w3_stage[a][:], w3_raw[a][:], "scalar"), BANK, "w3_%d" % a)
 
         w3_q = [quantize_w3(0)]
-        for t in range(2, PACK):
-            gather(x0[:, t, :], 0, t, 0, S)
+        second_wholes = [terms[:, 1, :]] + [as_floats(stage[i][:], 1) for i in range(PACK - 1)]
         for t in range(PACK):
-            fracs[t] = reduce_on_tensor(t, *second_terms[t])
-            if t < PACK - 1:
-                scatter(1, t, sine(sines[t], fracs[t]))
+            scatter(1, t, sine(sines[t], reduce_on_tensor(t, w3_raw[0][:, t, :], second_wholes[t])))
         w3_q += [quantize_w3(a) for a in range(1, K_PASSES)]
         x0_q = quantize(weave(stage[2][:], x0[:], "scalar"), BANK, "x0")
-        last_sine = sine(x0[:, 0, :], fracs[PACK - 1])
-        scale_wgt(1, w3_raw[K_PASSES - 1])
-        scatter(1, PACK - 1, last_sine)
 
         banks = {}
         for c, (start, width) in enumerate(CHUNKS):
@@ -370,19 +363,26 @@ def tile_list_antiskid_valve_features_kernel(
             cols = slice(start, start + width)
             w4_pass(c, 0, x0_q[0][:, cols], x0_q[1][:, cols])
 
-        x1_bytes = [last_sine, wgs_gain[1, 3]] * 2
-        x1_rounded = [stage[c][:, :S] for c in range(len(CHUNKS))]
+        x1_bytes = [sines[3], wgs_gain[1, 3]] * 2
+        x1_rounded = [stage[c][:, 2 * S : 3 * S] for c in range(len(CHUNKS))]
         out_view = out.rearrange("(a p) m -> p a m", p=P)
+
+        def finish_chunk(c):
+            codes, scales = quantize(x1_rounded[c], CHUNKS[c][1], "x1_%d" % c)
+            w4_pass(c, 1, codes[:], scales[:])
+
         for c, (start, width) in enumerate(CHUNKS):
             x1 = x1_bytes[c].rearrange("p (t c) -> p t c", t=PACK)
             for t in range(PACK):
                 gather(x1[:, t, :], 1, t, start, width)
-            rounded = weave(x1_rounded[c], x1, "vector" if c >= 2 else "scalar")
-            codes, scales = quantize(rounded, width, "x1_%d" % c)
-            w4_pass(c, 1, codes[:], scales[:])
+            if c > 0:
+                finish_chunk(c - 1)
+            weave(x1_rounded[c], x1, "vector" if c == len(CHUNKS) - 1 else "scalar")
+        finish_chunk(len(CHUNKS) - 1)
         for c, (start, width) in enumerate(CHUNKS):
             result = ring.tile([P, N_TILES, width], F32, name="result", tag="raw", bufs=6)
             for n in range(N_TILES):
                 bank, i = banks[c, n][:2]
                 nc.scalar.activation(out=result[:, n, :], in_=bank[:, i, :], func=ACT.Tanh, bias=bias_t[:, n : n + 1])
-            nc.sync.dma_start(out=out_view[:, :, start : start + width], in_=result[:])
+            for tiles in (slice(0, 2), slice(2, 4)) if c == len(CHUNKS) - 1 else (slice(0, 4),):
+                nc.sync.dma_start(out=out_view[:, tiles, start : start + width], in_=result[:, tiles, :])

@@ -23,12 +23,23 @@ PACK = 4
 PASS = P * PACK
 K_PASSES = K // PASS
 H_PASSES = H // PASS
+BLOCKS = S // P
 N_TILES = N // P
-BANK = 512
+QUADRANTS = 4
+QUADRANT = P // QUADRANTS
+SCALE_ROWS = 4
+GROUP = 16
+RUN = 4
+RAW_BUFS = 6
 TWO_PI = 2.0 * math.pi
 ROUNDER = 1.5 * 2.0**23
+ALL = slice(0, S)
 HALVES = (slice(0, S // 2), slice(S // 2, S))
-CHUNKS = ((0, 128), (128, 128), (256, 128), (384, 128))
+CHUNKS = S // P
+
+
+def block(i):
+    return slice(P * i, P * (i + 1))
 
 
 def tile_list_antiskid_valve_features_kernel(
@@ -44,104 +55,96 @@ def tile_list_antiskid_valve_features_kernel(
         w4_plane = held.tile([P, H_PASSES, N], U8, name="w4_plane", align_bytes=64)
         nc.vector.memset(tab_plane[:].bitcast(I32), 0)
         nc.vector.memset(w4_plane[:].bitcast(I32), 0)
-        valve_t = held.tile([P, H_PASSES, PACK], F32, name="valve_t")
-        gain_t = held.tile([P, H_PASSES, PACK], F32, name="gain_t")
+        valve_t = held.tile([P, H_PASSES, 2 * PACK], F32, name="valve_t")
+        gain_t = held.tile([P, H_PASSES, 2 * PACK], F32, name="gain_t")
         bias_t = held.tile([P, N_TILES], F32, name="bias_t")
-
-        list1 = held.tile([P, S // 16], U16, name="list1")
-        list2 = held.tile([P, S // 16], U16, name="list2")
-        list3 = held.tile([P, S // 16], U16, name="list3")
-
-        def load_rows(src):
-            raw = ring.tile([P, PACK, BANK], F32, name="raw", tag="raw", bufs=6)
-            nc.sync.dma_start(out=raw[:], in_=src.rearrange("(p j) c -> p j c", j=PACK))
-            return raw
-
-        def load_page(b, t):
-            page = held.tile([P, T2], F32, name="page%d%d" % (b, t))
-            rows = page0[PASS * b : PASS * (b + 1), :].rearrange("(p t) c -> p t c", t=PACK)
-            nc.sync.dma_start(out=page[:], in_=rows[:, t, :])
-            return page
-
-        def w1_rows(b, a):
-            return w1[PASS * a : PASS * (a + 1), PASS * b : PASS * (b + 1)]
-
-        w1_raw = {}
-        tab = []
+        list1 = held.tile([P, S // GROUP], U16, name="list1")
+        list2 = held.tile([P, S // GROUP], U16, name="list2")
+        list3 = held.tile([P, S // GROUP], U16, name="list3")
         wgt_t = held.tile([P, S], F32, name="wgt_t")
         wgs_t = held.tile([P, S], F32, name="wgs_t")
+        w1_raw, pages, tab = {}, {}, []
+
+        def load_rows(src):
+            raw = ring.tile([P, PACK, PASS], F32, name="raw", tag="raw", bufs=RAW_BUFS)
+            nc.sync.dma_start(out=raw[:], in_=src.rearrange("(p i) c -> p i c", i=PACK))
+            return raw
+
+        def load_w1(b, a):
+            w1_raw[b, a] = load_rows(w1[PASS * a : PASS * (a + 1), PASS * b : PASS * (b + 1)])
 
         def load_table(a):
             words = held.tile([P, T], U32, name="tab%d" % a)
             nc.sync.dma_start(out=words[:].bitcast(I32), in_=tab_words[a].rearrange("p t i -> p (t i)").bitcast(I32))
             tab.append(words)
 
+        def load_page(b, t):
+            page = held.tile([P, T2], F32, name="page%d%d" % (b, t))
+            rows = page0[PASS * b : PASS * (b + 1), :].rearrange("(p t) c -> p t c", t=PACK)
+            nc.sync.dma_start(out=page[:], in_=rows[:, t, :])
+            pages[b, t] = page
+
+        def load_row_factors(dst, src):
+            nc.sync.dma_start(out=dst[:, :, :PACK], in_=src.rearrange("(b p t) -> p b t", b=H_PASSES, t=PACK))
+
         nc.sync.dma_start(out=wgs_t[:], in_=wgs)
-        w1_raw[0, 0] = load_rows(w1_rows(0, 0))
-        nc.sync.dma_start(out=gain_t[:], in_=gain.rearrange("(b p t) -> p b t", b=H_PASSES, t=PACK))
+        load_w1(0, 0)
+        load_row_factors(gain_t, gain)
         load_table(0)
         nc.sync.dma_start(list1[:], offs)
-        for q in range(4):
+        for q in range(QUADRANTS):
             nc.sync.dma_start(
-                out=tab_plane[32 * q : 32 * q + 4 * K_PASSES, :].bitcast(I32),
-                in_=tab_scales[:, 4 * q : 4 * q + 4, :].bitcast(I32),
+                out=tab_plane[QUADRANT * q : QUADRANT * q + SCALE_ROWS * K_PASSES, :].bitcast(I32),
+                in_=tab_scales[:, SCALE_ROWS * q : SCALE_ROWS * (q + 1), :].bitcast(I32),
             )
-        w1_raw[0, 1] = load_rows(w1_rows(0, 1))
+        load_w1(0, 1)
         nc.sync.dma_start(out=wgt_t[:], in_=wgt)
-        nc.sync.dma_start(out=valve_t[:], in_=valve.rearrange("(b p t) -> p b t", b=H_PASSES, t=PACK))
+        load_row_factors(valve_t, valve)
         load_table(1)
-        w1_raw[0, 2] = load_rows(w1_rows(0, 2))
+        load_w1(0, 2)
         load_table(2)
         nc.sync.dma_start(list2[:], offs2)
-        pages = {}
-        pages[0, 0] = load_page(0, 0)
+        load_page(0, 0)
         nc.sync.dma_start(list3[:], offs3)
-        pages[0, 1] = load_page(0, 1)
+        load_page(0, 1)
         for a in range(K_PASSES):
-            w1_raw[1, a] = load_rows(w1_rows(1, a))
-        w3_raw = [load_rows(w3[PASS * a : PASS * (a + 1), :]) for a in range(K_PASSES - 1)]
-        pages[0, 2] = load_page(0, 2)
-        pages[0, 3] = load_page(0, 3)
-        w3_raw.append(load_rows(w3[PASS * (K_PASSES - 1) :, :]))
-        pages[1, 0] = load_page(1, 0)
-        pages[1, 1] = load_page(1, 1)
+            load_w1(1, a)
+        load_page(0, 2)
+        load_page(0, 3)
+        w3_raw = [load_rows(w3[PASS * a : PASS * (a + 1), :]) for a in range(K_PASSES)]
+        load_page(1, 0)
+        load_page(1, 1)
         w4_t = held.tile([P, H_PASSES, 2 * N], U8, name="w4_t", align_bytes=64)
-        nc.sync.dma_start(out=w4_t[:].bitcast(I32), in_=w4_words.rearrange("a p c -> p a c").bitcast(I32))
-        pages[1, 2] = load_page(1, 2)
-        pages[1, 3] = load_page(1, 3)
-        for q in range(4):
+        nc.sync.dma_start(out=w4_t[:].bitcast(I32), in_=w4_words.rearrange("b p c -> p b c").bitcast(I32))
+        load_page(1, 2)
+        load_page(1, 3)
+        for q in range(QUADRANTS):
             nc.sync.dma_start(
-                out=w4_plane[32 * q : 32 * q + 4, :, :].bitcast(I32),
-                in_=w4_scales[:, 4 * q : 4 * q + 4, :].rearrange("a r c -> r a c").bitcast(I32),
+                out=w4_plane[QUADRANT * q : QUADRANT * q + SCALE_ROWS, :, :].bitcast(I32),
+                in_=w4_scales[:, SCALE_ROWS * q : SCALE_ROWS * (q + 1), :].rearrange("b r c -> r b c").bitcast(I32),
             )
-        with nc.allow_non_contiguous_dma(reason="one bias value for each partition"):
-            nc.sync.dma_start(out=bias_t[:], in_=bias.rearrange("(a p) -> p a", p=P))
+        with nc.allow_non_contiguous_dma(reason="one bias value for each partition and output tile"):
+            nc.sync.dma_start(out=bias_t[:], in_=bias.rearrange("(n p) -> p n", p=P))
 
-        def copy_on(engine):
-            return nc.vector.tensor_copy if engine == "vector" else nc.scalar.copy
+        stage = [held.tile([P, PACK * PASS], BF16, name="stage%d" % i, align_bytes=64) for i in range(PACK)]
 
-        stage = [held.tile([P, PACK * BANK], BF16, name="stage%d" % i, align_bytes=64) for i in range(4)]
+        def lent(i, half):
+            return stage[i][:].bitcast(F32)[:, S * half : S * (half + 1)]
 
         def entries(offsets, cols):
-            return offsets[:, cols.start // 16 : cols.stop // 16]
+            return offsets[:, cols.start // GROUP : cols.stop // GROUP]
 
-        def as_floats(ap, index):
-            return ap.bitcast(F32)[:, S * index : S * (index + 1)]
-
-        def weave_w1(rounded, raw, engines):
-            share = PACK // len(engines)
-            for i, engine in enumerate(engines):
-                part = slice(share * i, share * (i + 1))
-                copy_on(engine)(
-                    out=rounded.rearrange("p (t m j) -> p m j t", t=PACK, j=PACK)[:, :, :, part],
-                    in_=raw[:].rearrange("p j (m t) -> p m j t", t=PACK)[:, :, :, part],
-                )
+        def interleave_w1(copy, rounded, raw):
+            copy(
+                out=rounded.rearrange("k (t p i) -> k p i t", t=PACK, i=PACK),
+                in_=raw[:].rearrange("k i (p t) -> k p i t", t=PACK),
+            )
             return rounded
 
-        def weave(rounded, raw, engine):
-            copy_on(engine)(
-                out=rounded.rearrange("p (c i j) -> p c j i", i=4, j=PACK),
-                in_=raw.rearrange("p j (c i) -> p c j i", i=4),
+        def interleave(copy, rounded, rows):
+            copy(
+                out=rounded.rearrange("k (c e i) -> k c i e", e=RUN, i=PACK),
+                in_=rows.rearrange("k i (c e) -> k c i e", e=RUN),
             )
             return rounded
 
@@ -155,234 +158,188 @@ def tile_list_antiskid_valve_features_kernel(
             nc.scalar.activation(out=dst, in_=src, func=ACT.Copy, scale=factor)
             return dst
 
-        sums = [psum.tile([P, BANK], F32, name="sums%d" % t) for t in range(PACK)]
-        turned = [psum.tile([P, BANK], F32, name="turned%d" % t) for t in range(PACK)]
+        sums = [psum.tile([P, PASS], F32, name="sums%d" % t) for t in range(PACK)]
+        turned = [psum.tile([P, PASS], F32, name="turned%d" % t) for t in range(PACK)]
         identity = held.tile([P, P], F32, name="identity")
         make_identity(nc, identity[:])
+
+        def transpose(dst, src, start=True, stop=True):
+            nc.tensor.matmul(dst, src, identity[:], start=start, stop=stop, is_transpose=True)
+
         x0 = held.tile([P, PACK, S], F32, name="x0", align_bytes=64)
         warm = held.tile([P, 8], F32, name="warm")
         nc.scalar.activation(out=warm[:, 0:1], in_=identity[:, 0:1], func=ACT.Silu)
 
-        def block(i):
-            return slice(P * i, P * (i + 1))
-
-        for jb in range(S // P):
-            nc.tensor.matmul(turned[0][:, block(jb)], wgs_t[:, block(jb)], identity[:], start=True, stop=True, is_transpose=True)
-        wgs_turned = x0[:].rearrange("p jb (t rep q) -> p jb t rep q", t=PACK, rep=4)
-        for rep in range(4):
-            nc.scalar.copy(out=wgs_turned[:, :, :, rep, :], in_=turned[0][:].rearrange("p (jb q t) -> p jb t q", t=PACK, jb=S // P))
-        wgs_gain = {}
+        for j in range(BLOCKS):
+            transpose(turned[0][:, block(j)], wgs_t[:, block(j)])
+        wgs_sorted = x0[:].rearrange("k j (t q p) -> k j t q p", t=PACK, q=QUADRANTS)
+        for q in range(QUADRANTS):
+            nc.scalar.copy(
+                out=wgs_sorted[:, :, :, q, :], in_=turned[0][:].rearrange("k (j p t) -> k j t p", t=PACK, j=BLOCKS)
+            )
+        wgs_gain, wgt_valve = {}, {}
         for t in range(PACK):
-            for jb in range(S // P):
-                nc.tensor.matmul(sums[t][:, block(jb)], x0[:, jb, block(t)], identity[:], start=True, stop=True, is_transpose=True)
+            for j in range(BLOCKS):
+                transpose(sums[t][:, block(j)], x0[:, j, block(t)])
             for b in range(H_PASSES):
                 dst = held.tile([P, S], F32, name="wgs_gain%d%d" % (b, t))
                 wgs_gain[b, t] = scaled(dst[:], sums[t][:], gain_t[:, b, t : t + 1])
-
-        wgt_valve = {}
-
-        def scale_wgt(b, dst):
+        for b in range(H_PASSES):
+            dst = held.tile([P, PACK, S], F32, name="wgt_valve%d" % b)
             for t in range(PACK):
                 wgt_valve[b, t] = scaled(dst[:, t, :], wgt_t[:], valve_t[:, b, t : t + 1])
 
-        for b in range(H_PASSES):
-            scale_wgt(b, held.tile([P, PACK, S], F32, name="wgt_valve%d" % b))
-
         v_scales = held.tile([P, S], U8, name="v_scales", align_bytes=64)
-        v_codes = []
-        w1_q = {}
+        v_codes, w1_q = [], {}
         for a in range(K_PASSES):
-            w1_q[0, a] = quantize(weave_w1(stage[a][:], w1_raw[0, a], ("vector",)), BANK, "w1_0%d" % a)
+            rounded = interleave_w1(nc.vector.tensor_copy, stage[a][:], w1_raw[0, a])
+            w1_q[0, a] = quantize(rounded, PASS, "w1_0%d" % a)
             if a == 0:
                 nc.vector.tensor_copy(v_scales[:], tab_plane[:].indirect(list1[:]))
             picked = held.tile([P, S], U32, name="v_codes%d" % a, align_bytes=64)
-            for cols in HALVES if a == K_PASSES - 1 else (slice(0, S),):
+            for cols in HALVES if a == K_PASSES - 1 else (ALL,):
                 nc.vector.tensor_copy(picked[:, cols], tab[a][:].indirect(entries(list1, cols)))
             v_codes.append(picked)
 
-        def first_product(b, direct):
+        def v_operand(a, cols):
+            return v_codes[a][:, cols].bitcast(FP8X4), v_scales[SCALE_ROWS * a :, cols]
+
+        def multiply(dst, stationary, moving, start, stop):
+            nc.tensor.matmul_mx(
+                out=dst,
+                lhsT=stationary[0],
+                lhsT_scale=stationary[1],
+                rhs=moving[0],
+                rhs_scale=moving[1],
+                start=start,
+                stop=stop,
+            )
+
+        def columns(quantized, cols):
+            return quantized[0][:, cols].bitcast(FP8X4), quantized[1][:, cols]
+
+        first_halves = [(bank[:, cols], cols) for bank, cols in zip((sums[0], turned[0]), HALVES)]
+
+        def first_product(b):
             for a in range(K_PASSES):
-                codes, scales = w1_q[b, a]
                 first, last = a == 0, a == K_PASSES - 1
                 for t in range(PACK):
-                    if t in direct:
-                        for bank, cols in zip((sums[t], turned[t]), HALVES):
-                            nc.tensor.matmul_mx(
-                                out=bank[:, cols],
-                                lhsT=codes[:, block(t)].bitcast(FP8X4),
-                                lhsT_scale=scales[:, block(t)],
-                                rhs=v_codes[a][:, cols].bitcast(FP8X4),
-                                rhs_scale=v_scales[4 * a :, cols],
-                                start=first,
-                                stop=last,
-                            )
-                        continue
-                    for jb in range(S // P):
-                        nc.tensor.matmul_mx(
-                            out=sums[t][:, block(jb)],
-                            lhsT=v_codes[a][:, block(jb)].bitcast(FP8X4),
-                            lhsT_scale=v_scales[4 * a :, block(jb)],
-                            rhs=codes[:, block(t)].bitcast(FP8X4),
-                            rhs_scale=scales[:, block(t)],
-                            start=first and jb == 0,
-                            stop=last and jb == S // P - 1,
-                        )
+                    weights = columns(w1_q[b, a], block(t))
+                    if (b, t) == (0, 0):
+                        for z, cols in first_halves:
+                            multiply(z, weights, v_operand(a, cols), first, last)
+                    else:
+                        for j in range(BLOCKS):
+                            opens, closes = first and j == 0, last and j == BLOCKS - 1
+                            multiply(sums[t][:, block(j)], v_operand(a, block(j)), weights, opens, closes)
 
-        sine_tiles = [held.tile([P, S], F32, name="sine%d" % t) for t in range(PACK)]
-        sines = [tile[:] for tile in sine_tiles]
-
+        sines = [held.tile([P, S], F32, name="sine%d" % t) for t in range(PACK)]
         terms = held.tile([P, 3, S], F32, name="terms")
         biased_first = held.tile([P, S], I32, name="biased_first")
 
-        def reduce_on_vector(z, cols):
-            frac, whole = as_floats(stage[0][:], 0)[:, cols], as_floats(stage[0][:], 1)[:, cols]
-            biased = biased_first[:, cols]
+        def fraction_on_vector(z, cols):
+            fraction, whole, biased = lent(0, 0)[:, cols], lent(0, 1)[:, cols], biased_first[:, cols]
             nc.vector.tensor_scalar(
                 out=biased, in0=z, scalar1=1.0 / TWO_PI, scalar2=ROUNDER, op0=ALU.mult, op1=ALU.add
             )
             nc.vector.tensor_scalar(out=whole, in0=biased, scalar1=-ROUNDER, scalar2=None, op0=ALU.add)
             nc.vector.scalar_tensor_tensor(
-                out=frac, in0=z, scalar=1.0 / TWO_PI, in1=whole, op0=ALU.mult, op1=ALU.subtract
+                out=fraction, in0=z, scalar=1.0 / TWO_PI, in1=whole, op0=ALU.mult, op1=ALU.subtract
             )
-            return frac
+            return fraction
 
-        def reduce_on_tensor(t, turns, minus_whole):
+        def fraction_by_transposes(t, turns, minus_whole):
             biased = ring.tile([P, S], U32, name="biased", tag="biased")
             nc.scalar.activation(out=turns, in_=sums[t][:], func=ACT.Copy, scale=1.0 / TWO_PI)
             nc.scalar.activation(out=biased[:], in_=turns, func=ACT.Copy, scale=1.0, bias=ROUNDER)
             nc.scalar.activation(out=minus_whole, in_=biased[:], func=ACT.Copy, scale=-1.0, bias=ROUNDER)
-            for i, term in enumerate((turns, minus_whole)):
-                for jb in range(S // P):
-                    nc.tensor.matmul(
-                        turned[t][:, block(jb)],
-                        term[:, block(jb)],
-                        identity[:],
-                        start=(i == 0 and jb == 0),
-                        stop=(i == 1 and jb == S // P - 1),
-                        is_transpose=True,
-                    )
+            for term, opens in ((turns, True), (minus_whole, False)):
+                for j in range(BLOCKS):
+                    closes = not opens and j == BLOCKS - 1
+                    transpose(turned[t][:, block(j)], term[:, block(j)], opens and j == 0, closes)
             return turned[t][:]
 
-        def sine(dst, frac):
-            nc.scalar.activation(out=dst, in_=frac, func=ACT.Sin, scale=TWO_PI)
+        def sine(dst, fraction):
+            nc.scalar.activation(out=dst, in_=fraction, func=ACT.Sin, scale=TWO_PI)
             return dst
 
-        def scatter(b, t, sin_z, cols=slice(0, S)):
-            nc.vector.tensor_tensor(
-                pages[b, t][:].indirect(entries(list2, cols)), sin_z, wgs_gain[b, t][:, cols], ALU.mult
-            )
+        def scatter(b, t, sin_z, cols):
+            window = pages[b, t][:].indirect(entries(list2, cols))
+            nc.vector.tensor_tensor(window, sin_z, wgs_gain[b, t][:, cols], ALU.mult)
 
-        def gather(dst, b, t, start, width):
-            offsets = list3[:, start // 16 : (start + width) // 16]
-            nc.vector.tensor_tensor(
-                dst, pages[b, t][:].indirect(offsets), wgt_valve[b, t][:, start : start + width], ALU.mult
-            )
+        def gather(dst, b, t, cols):
+            window = pages[b, t][:].indirect(entries(list3, cols))
+            nc.vector.tensor_tensor(dst, window, wgt_valve[b, t][:, cols], ALU.mult)
 
-        first_product(0, (0,))
-        first_fracs = [reduce_on_vector(bank[:, cols], cols) for bank, cols in zip((sums[0], turned[0]), HALVES)]
-        for frac, cols in zip(first_fracs, HALVES):
-            scatter(0, 0, sine(as_floats(stage[1][:], 0)[:, cols], frac), cols)
-        first_terms = {
-            1: (terms[:, 0, :], terms[:, 1, :]),
-            2: (terms[:, 2, :], as_floats(stage[0][:], 1)),
-            3: (as_floats(stage[2][:], 0), x0[:, 2, :]),
+        first_product(0)
+        first_fractions = [fraction_on_vector(z, cols) for z, cols in first_halves]
+        for fraction, cols in zip(first_fractions, HALVES):
+            scatter(0, 0, sine(lent(1, 0)[:, cols], fraction), cols)
+        scatter(0, 1, sine(sines[1][:], fraction_by_transposes(1, terms[:, 0, :], terms[:, 1, :])), ALL)
+        late_fractions = {
+            2: fraction_by_transposes(2, terms[:, 2, :], lent(0, 1)),
+            3: fraction_by_transposes(3, lent(2, 0), x0[:, 2, :]),
         }
-        for t in range(1, PACK - 1):
-            scatter(0, t, sine(sines[t], reduce_on_tensor(t, *first_terms[t])))
-        last_frac = reduce_on_tensor(PACK - 1, *first_terms[PACK - 1])
-        w1_stage = (stage[0][:], stage[2][:], x0[:, 2:4, :].rearrange("p t c -> p (t c)").bitcast(BF16))
+        w1_stage = (stage[0][:], stage[2][:], x0[:, 2:, :].rearrange("k t c -> k (t c)").bitcast(BF16))
+        scatter_after = {0: 2, K_PASSES - 1: 3}
         for a in range(K_PASSES):
-            w1_q[1, a] = quantize(weave_w1(w1_stage[a], w1_raw[1, a], ("scalar",)), BANK, "w1_1%d" % a)
-        scatter(0, PACK - 1, sine(w1_raw[1, K_PASSES - 1][:, 0, :], last_frac))
-        first_product(1, ())
+            w1_q[1, a] = quantize(interleave_w1(nc.scalar.copy, w1_stage[a], w1_raw[1, a]), PASS, "w1_1%d" % a)
+            if a in scatter_after:
+                t = scatter_after[a]
+                scatter(0, t, sine(w1_raw[1, a][:, 0, :], late_fractions[t]), ALL)
+        first_product(1)
         for t in range(PACK):
-            gather(x0[:, t, :], 0, t, 0, S)
+            gather(x0[:, t, :], 0, t, ALL)
 
-        w3_stage = (stage[3], stage[0], stage[1])
+        w3_stage = (stage[3][:], stage[0][:], stage[1][:])
 
         def quantize_w3(a):
-            return quantize(weave(w3_stage[a][:], w3_raw[a][:], "scalar"), BANK, "w3_%d" % a)
+            return quantize(interleave(nc.scalar.copy, w3_stage[a], w3_raw[a][:]), PASS, "w3_%d" % a)
 
         w3_q = [quantize_w3(0)]
-        second_wholes = [terms[:, 1, :]] + [as_floats(stage[i][:], 1) for i in range(PACK - 1)]
+        wholes = [terms[:, 1, :]] + [lent(i, 1) for i in range(PACK - 1)]
         for t in range(PACK):
-            scatter(1, t, sine(sines[t], reduce_on_tensor(t, w3_raw[0][:, t, :], second_wholes[t])))
+            scatter(1, t, sine(sines[t][:], fraction_by_transposes(t, w3_raw[0][:, t, :], wholes[t])), ALL)
         w3_q += [quantize_w3(a) for a in range(1, K_PASSES)]
-        x0_q = quantize(weave(stage[2][:], x0[:], "scalar"), BANK, "x0")
+        x0_q = quantize(interleave(nc.scalar.copy, stage[2][:], x0[:]), PASS, "x0")
 
-        banks = {}
-        for c, (start, width) in enumerate(CHUNKS):
-            per_bank = BANK // width
-            for g in range(N_TILES // per_bank):
-                bank = turned[c][:].rearrange("p (i c) -> p i c", i=per_bank)
-                for i in range(per_bank):
-                    banks[c, g * per_bank + i] = (bank, i, i == 0, i == per_bank - 1)
-
-        def output_pass(c, n, lhsT, lhsT_scale, rhs, rhs_scale, first, last):
-            bank, i, opens, closes = banks[c, n]
-            nc.tensor.matmul_mx(
-                out=bank[:, i, :],
-                lhsT=lhsT,
-                lhsT_scale=lhsT_scale,
-                rhs=rhs,
-                rhs_scale=rhs_scale,
-                start=first and opens,
-                stop=last and closes,
-            )
-
-        def w4_pass(c, b, codes, scales):
+        def w4_pass(c, b, x_operand):
             for n in range(N_TILES):
-                output_pass(
-                    c,
-                    n,
-                    w4_t[:, b, 2 * P * n : 2 * P * (n + 1)].bitcast(FP4X4),
-                    w4_plane[:, b, P * n : P * (n + 1)],
-                    codes.bitcast(FP8X4),
-                    scales,
-                    False,
-                    b == H_PASSES - 1,
-                )
+                weights = w4_t[:, b, 2 * P * n : 2 * P * (n + 1)].bitcast(FP4X4), w4_plane[:, b, block(n)]
+                closes = b == H_PASSES - 1 and n == N_TILES - 1
+                multiply(turned[c][:, block(n)], weights, x_operand, False, closes)
 
         for a in range(K_PASSES):
-            codes, scales = w3_q[a]
-            for c, (start, width) in enumerate(CHUNKS):
-                cols = slice(start, start + width)
+            for c in range(CHUNKS):
                 for n in range(N_TILES):
-                    rows = slice(P * n, P * (n + 1))
-                    output_pass(
-                        c,
-                        n,
-                        codes[:, rows].bitcast(FP8X4),
-                        scales[:, rows],
-                        v_codes[a][:, cols].bitcast(FP8X4),
-                        v_scales[4 * a :, cols],
-                        a == 0,
-                        False,
-                    )
-        for c, (start, width) in enumerate(CHUNKS):
-            cols = slice(start, start + width)
-            w4_pass(c, 0, x0_q[0][:, cols], x0_q[1][:, cols])
+                    opens = a == 0 and n == 0
+                    multiply(turned[c][:, block(n)], columns(w3_q[a], block(n)), v_operand(a, block(c)), opens, False)
+        for c in range(CHUNKS):
+            w4_pass(c, 0, columns(x0_q, block(c)))
 
-        x1_bytes = [sines[3], wgs_gain[1, 3]] * 2
-        x1_rounded = [stage[c][:, 2 * S : 3 * S] for c in range(len(CHUNKS))]
-        out_view = out.rearrange("(a p) m -> p a m", p=P)
+        x1_bytes = (sines[PACK - 1][:], wgs_gain[1, PACK - 1])
+        x1_rounded = [stage[c][:, 2 * S : 3 * S] for c in range(CHUNKS)]
 
         def finish_chunk(c):
-            codes, scales = quantize(x1_rounded[c], CHUNKS[c][1], "x1_%d" % c)
-            w4_pass(c, 1, codes[:], scales[:])
+            w4_pass(c, 1, columns(quantize(x1_rounded[c], P, "x1_%d" % c), slice(0, P)))
 
-        for c, (start, width) in enumerate(CHUNKS):
-            x1 = x1_bytes[c].rearrange("p (t c) -> p t c", t=PACK)
+        for c in range(CHUNKS):
+            x1 = x1_bytes[c % 2].rearrange("k (t m) -> k t m", t=PACK)
             for t in range(PACK):
-                gather(x1[:, t, :], 1, t, start, width)
+                gather(x1[:, t, :], 1, t, block(c))
             if c > 0:
                 finish_chunk(c - 1)
-            weave(x1_rounded[c], x1, "vector" if c == len(CHUNKS) - 1 else "scalar")
-        finish_chunk(len(CHUNKS) - 1)
-        for c, (start, width) in enumerate(CHUNKS):
-            result = ring.tile([P, N_TILES, width], F32, name="result", tag="raw", bufs=6)
+            interleave(nc.vector.tensor_copy if c == CHUNKS - 1 else nc.scalar.copy, x1_rounded[c], x1)
+        finish_chunk(CHUNKS - 1)
+
+        out_view = out.rearrange("(n p) m -> p n m", p=P)
+        for c in range(CHUNKS):
+            result = ring.tile([P, N_TILES, P], F32, name="result", tag="raw", bufs=RAW_BUFS)
             for n in range(N_TILES):
-                bank, i = banks[c, n][:2]
-                nc.scalar.activation(out=result[:, n, :], in_=bank[:, i, :], func=ACT.Tanh, bias=bias_t[:, n : n + 1])
-            for tiles in (slice(0, 2), slice(2, 4)) if c == len(CHUNKS) - 1 else (slice(0, 4),):
-                nc.sync.dma_start(out=out_view[:, tiles, start : start + width], in_=result[:, tiles, :])
+                nc.scalar.activation(
+                    out=result[:, n, :], in_=turned[c][:, block(n)], func=ACT.Tanh, bias=bias_t[:, n : n + 1]
+                )
+            parts = 2 if c == CHUNKS - 1 else 1
+            for part in range(parts):
+                tiles = slice(part * N_TILES // parts, (part + 1) * N_TILES // parts)
+                nc.sync.dma_start(out=out_view[:, tiles, block(c)], in_=result[:, tiles, :])

import math
from contextlib import ExitStack

import concourse.mybir as mybir
from concourse.masks import make_identity

K, T, S, H, T2, N = 1536, 2048, 512, 1024, 1024, 512
FLOPS = 2 * (K * H * S + H * N * S + K * N * S)

F32 = mybir.dt.float32
BF16 = mybir.dt.bfloat16
I32 = mybir.dt.int32
U32 = mybir.dt.uint32
U16 = mybir.dt.uint16
U8 = mybir.dt.uint8
FP8X4 = mybir.dt.float8_e4m3fn_x4
FP4X4 = mybir.dt.float4_e2m1fn_x4
ACT = mybir.ActivationFunctionType
ALU = mybir.AluOpType

P = 128
PACK = 4
PASS = P * PACK
K_PASSES = K // PASS
H_PASSES = H // PASS
BLOCKS = S // P
N_TILES = N // P
QUADRANTS = 4
QUADRANT = P // QUADRANTS
SCALE_ROWS = 4
GROUP = 16
RUN = 4
RAW_BUFS = 6
TWO_PI = 2.0 * math.pi
ROUNDER = 1.5 * 2.0**23
ALL = slice(0, S)
HALVES = (slice(0, S // 2), slice(S // 2, S))
CHUNKS = S // P


def block(i):
    return slice(P * i, P * (i + 1))


def tile_list_antiskid_valve_features_kernel(
    tc, tab_words, tab_scales, offs, w1, gain, page0, wgs, offs2, wgt, offs3, valve, w4_words, w4_scales, w3, bias, out
):
    nc = tc.nc
    with ExitStack() as ctx:
        held = ctx.enter_context(tc.tile_pool(name="held", bufs=1))
        ring = ctx.enter_context(tc.tile_pool(name="ring", bufs=2))
        psum = ctx.enter_context(tc.psum_pool(name="psum", bufs=1))

        tab_plane = held.tile([P, T], U8, name="tab_plane", align_bytes=64)
        w4_plane = held.tile([P, H_PASSES, N], U8, name="w4_plane", align_bytes=64)
        nc.vector.memset(tab_plane[:].bitcast(I32), 0)
        nc.vector.memset(w4_plane[:].bitcast(I32), 0)
        valve_t = held.tile([P, H_PASSES, 2 * PACK], F32, name="valve_t")
        gain_t = held.tile([P, H_PASSES, 2 * PACK], F32, name="gain_t")
        bias_t = held.tile([P, N_TILES], F32, name="bias_t")
        list1 = held.tile([P, S // GROUP], U16, name="list1")
        list2 = held.tile([P, S // GROUP], U16, name="list2")
        list3 = held.tile([P, S // GROUP], U16, name="list3")
        wgt_t = held.tile([P, S], F32, name="wgt_t")
        wgs_t = held.tile([P, S], F32, name="wgs_t")
        w1_raw, pages, tab = {}, {}, []

        def load_rows(src):
            raw = ring.tile([P, PACK, PASS], F32, name="raw", tag="raw", bufs=RAW_BUFS)
            nc.sync.dma_start(out=raw[:], in_=src.rearrange("(p i) c -> p i c", i=PACK))
            return raw

        def load_w1(b, a):
            w1_raw[b, a] = load_rows(w1[PASS * a : PASS * (a + 1), PASS * b : PASS * (b + 1)])

        def load_table(a):
            words = held.tile([P, T], U32, name="tab%d" % a)
            nc.sync.dma_start(out=words[:].bitcast(I32), in_=tab_words[a].rearrange("p t i -> p (t i)").bitcast(I32))
            tab.append(words)

        def load_page(b, t):
            page = held.tile([P, T2], F32, name="page%d%d" % (b, t))
            rows = page0[PASS * b : PASS * (b + 1), :].rearrange("(p t) c -> p t c", t=PACK)
            nc.sync.dma_start(out=page[:], in_=rows[:, t, :])
            pages[b, t] = page

        def load_row_factors(dst, src):
            nc.sync.dma_start(out=dst[:, :, :PACK], in_=src.rearrange("(b p t) -> p b t", b=H_PASSES, t=PACK))

        nc.sync.dma_start(out=wgs_t[:], in_=wgs)
        load_w1(0, 0)
        load_row_factors(gain_t, gain)
        load_table(0)
        nc.sync.dma_start(list1[:], offs)
        for q in range(QUADRANTS):
            nc.sync.dma_start(
                out=tab_plane[QUADRANT * q : QUADRANT * q + SCALE_ROWS * K_PASSES, :].bitcast(I32),
                in_=tab_scales[:, SCALE_ROWS * q : SCALE_ROWS * (q + 1), :].bitcast(I32),
            )
        load_w1(0, 1)
        nc.sync.dma_start(out=wgt_t[:], in_=wgt)
        load_row_factors(valve_t, valve)
        load_table(1)
        load_w1(0, 2)
        load_table(2)
        nc.sync.dma_start(list2[:], offs2)
        load_page(0, 0)
        nc.sync.dma_start(list3[:], offs3)
        load_page(0, 1)
        for a in range(K_PASSES):
            load_w1(1, a)
        load_page(0, 2)
        load_page(0, 3)
        w3_raw = [load_rows(w3[PASS * a : PASS * (a + 1), :]) for a in range(K_PASSES)]
        load_page(1, 0)
        load_page(1, 1)
        w4_t = held.tile([P, H_PASSES, 2 * N], U8, name="w4_t", align_bytes=64)
        nc.sync.dma_start(out=w4_t[:].bitcast(I32), in_=w4_words.rearrange("b p c -> p b c").bitcast(I32))
        load_page(1, 2)
        load_page(1, 3)
        for q in range(QUADRANTS):
            nc.sync.dma_start(
                out=w4_plane[QUADRANT * q : QUADRANT * q + SCALE_ROWS, :, :].bitcast(I32),
                in_=w4_scales[:, SCALE_ROWS * q : SCALE_ROWS * (q + 1), :].rearrange("b r c -> r b c").bitcast(I32),
            )
        with nc.allow_non_contiguous_dma(reason="one bias value for each partition and output tile"):
            nc.sync.dma_start(out=bias_t[:], in_=bias.rearrange("(n p) -> p n", p=P))

        stage = [held.tile([P, PACK * PASS], BF16, name="stage%d" % i, align_bytes=64) for i in range(PACK)]

        def lent(i, half):
            return stage[i][:].bitcast(F32)[:, S * half : S * (half + 1)]

        def entries(offsets, cols):
            return offsets[:, cols.start // GROUP : cols.stop // GROUP]

        def interleave_w1(copy, rounded, raw):
            copy(
                out=rounded.rearrange("k (t p i) -> k p i t", t=PACK, i=PACK),
                in_=raw[:].rearrange("k i (p t) -> k p i t", t=PACK),
            )
            return rounded

        def interleave(copy, rounded, rows):
            copy(
                out=rounded.rearrange("k (c e i) -> k c i e", e=RUN, i=PACK),
                in_=rows.rearrange("k i (c e) -> k c i e", e=RUN),
            )
            return rounded

        def quantize(rounded, width, name):
            codes = held.tile([P, width], U32, name=name + "_codes", align_bytes=64)
            scales = held.tile([P, width], U8, name=name + "_scales", align_bytes=64)
            nc.vector.quantize_mx(out=codes[:].bitcast(FP8X4), scales=scales[:], in_=rounded)
            return codes, scales

        def scaled(dst, src, factor):
            nc.scalar.activation(out=dst, in_=src, func=ACT.Copy, scale=factor)
            return dst

        sums = [psum.tile([P, PASS], F32, name="sums%d" % t) for t in range(PACK)]
        turned = [psum.tile([P, PASS], F32, name="turned%d" % t) for t in range(PACK)]
        identity = held.tile([P, P], F32, name="identity")
        make_identity(nc, identity[:])

        def transpose(dst, src, start=True, stop=True):
            nc.tensor.matmul(dst, src, identity[:], start=start, stop=stop, is_transpose=True)

        x0 = held.tile([P, PACK, S], F32, name="x0", align_bytes=64)
        warm = held.tile([P, 8], F32, name="warm")
        nc.scalar.activation(out=warm[:, 0:1], in_=identity[:, 0:1], func=ACT.Silu)

        for j in range(BLOCKS):
            transpose(turned[0][:, block(j)], wgs_t[:, block(j)])
        wgs_sorted = x0[:].rearrange("k j (t q p) -> k j t q p", t=PACK, q=QUADRANTS)
        for q in range(QUADRANTS):
            nc.scalar.copy(
                out=wgs_sorted[:, :, :, q, :], in_=turned[0][:].rearrange("k (j p t) -> k j t p", t=PACK, j=BLOCKS)
            )
        wgs_gain, wgt_valve = {}, {}
        for t in range(PACK):
            for j in range(BLOCKS):
                transpose(sums[t][:, block(j)], x0[:, j, block(t)])
            for b in range(H_PASSES):
                dst = held.tile([P, S], F32, name="wgs_gain%d%d" % (b, t))
                wgs_gain[b, t] = scaled(dst[:], sums[t][:], gain_t[:, b, t : t + 1])
        for b in range(H_PASSES):
            dst = held.tile([P, PACK, S], F32, name="wgt_valve%d" % b)
            for t in range(PACK):
                wgt_valve[b, t] = scaled(dst[:, t, :], wgt_t[:], valve_t[:, b, t : t + 1])

        v_scales = held.tile([P, S], U8, name="v_scales", align_bytes=64)
        v_codes, w1_q = [], {}
        for a in range(K_PASSES):
            rounded = interleave_w1(nc.vector.tensor_copy, stage[a][:], w1_raw[0, a])
            w1_q[0, a] = quantize(rounded, PASS, "w1_0%d" % a)
            if a == 0:
                nc.vector.tensor_copy(v_scales[:], tab_plane[:].indirect(list1[:]))
            picked = held.tile([P, S], U32, name="v_codes%d" % a, align_bytes=64)
            for cols in HALVES if a == K_PASSES - 1 else (ALL,):
                nc.vector.tensor_copy(picked[:, cols], tab[a][:].indirect(entries(list1, cols)))
            v_codes.append(picked)

        def v_operand(a, cols):
            return v_codes[a][:, cols].bitcast(FP8X4), v_scales[SCALE_ROWS * a :, cols]

        def multiply(dst, stationary, moving, start, stop):
            nc.tensor.matmul_mx(
                out=dst,
                lhsT=stationary[0],
                lhsT_scale=stationary[1],
                rhs=moving[0],
                rhs_scale=moving[1],
                start=start,
                stop=stop,
            )

        def columns(quantized, cols):
            return quantized[0][:, cols].bitcast(FP8X4), quantized[1][:, cols]

        first_halves = [(bank[:, cols], cols) for bank, cols in zip((sums[0], turned[0]), HALVES)]

        def first_product(b):
            for a in range(K_PASSES):
                first, last = a == 0, a == K_PASSES - 1
                for t in range(PACK):
                    weights = columns(w1_q[b, a], block(t))
                    if (b, t) == (0, 0):
                        for z, cols in first_halves:
                            multiply(z, weights, v_operand(a, cols), first, last)
                    else:
                        for j in range(BLOCKS):
                            opens, closes = first and j == 0, last and j == BLOCKS - 1
                            multiply(sums[t][:, block(j)], v_operand(a, block(j)), weights, opens, closes)

        sines = [held.tile([P, S], F32, name="sine%d" % t) for t in range(PACK)]
        terms = held.tile([P, 3, S], F32, name="terms")
        biased_first = held.tile([P, S], I32, name="biased_first")

        def fraction_on_vector(z, cols):
            fraction, whole, biased = lent(0, 0)[:, cols], lent(0, 1)[:, cols], biased_first[:, cols]
            nc.vector.tensor_scalar(
                out=biased, in0=z, scalar1=1.0 / TWO_PI, scalar2=ROUNDER, op0=ALU.mult, op1=ALU.add
            )
            nc.vector.tensor_scalar(out=whole, in0=biased, scalar1=-ROUNDER, scalar2=None, op0=ALU.add)
            nc.vector.scalar_tensor_tensor(
                out=fraction, in0=z, scalar=1.0 / TWO_PI, in1=whole, op0=ALU.mult, op1=ALU.subtract
            )
            return fraction

        def fraction_by_transposes(t, turns, minus_whole):
            biased = ring.tile([P, S], U32, name="biased", tag="biased")
            nc.scalar.activation(out=turns, in_=sums[t][:], func=ACT.Copy, scale=1.0 / TWO_PI)
            nc.scalar.activation(out=biased[:], in_=turns, func=ACT.Copy, scale=1.0, bias=ROUNDER)
            nc.scalar.activation(out=minus_whole, in_=biased[:], func=ACT.Copy, scale=-1.0, bias=ROUNDER)
            for term, opens in ((turns, True), (minus_whole, False)):
                for j in range(BLOCKS):
                    closes = not opens and j == BLOCKS - 1
                    transpose(turned[t][:, block(j)], term[:, block(j)], opens and j == 0, closes)
            return turned[t][:]

        def sine(dst, fraction):
            nc.scalar.activation(out=dst, in_=fraction, func=ACT.Sin, scale=TWO_PI)
            return dst

        def scatter(b, t, sin_z, cols):
            window = pages[b, t][:].indirect(entries(list2, cols))
            nc.vector.tensor_tensor(window, sin_z, wgs_gain[b, t][:, cols], ALU.mult)

        def gather(dst, b, t, cols):
            window = pages[b, t][:].indirect(entries(list3, cols))
            nc.vector.tensor_tensor(dst, window, wgt_valve[b, t][:, cols], ALU.mult)

        first_product(0)
        first_fractions = [fraction_on_vector(z, cols) for z, cols in first_halves]
        for fraction, cols in zip(first_fractions, HALVES):
            scatter(0, 0, sine(lent(1, 0)[:, cols], fraction), cols)
        scatter(0, 1, sine(sines[1][:], fraction_by_transposes(1, terms[:, 0, :], terms[:, 1, :])), ALL)
        late_fractions = {
            2: fraction_by_transposes(2, terms[:, 2, :], lent(0, 1)),
            3: fraction_by_transposes(3, lent(2, 0), x0[:, 2, :]),
        }
        w1_stage = (stage[0][:], stage[2][:], x0[:, 2:, :].rearrange("k t c -> k (t c)").bitcast(BF16))
        scatter_after = {0: 2, K_PASSES - 1: 3}
        for a in range(K_PASSES):
            w1_q[1, a] = quantize(interleave_w1(nc.scalar.copy, w1_stage[a], w1_raw[1, a]), PASS, "w1_1%d" % a)
            if a in scatter_after:
                t = scatter_after[a]
                scatter(0, t, sine(w1_raw[1, a][:, 0, :], late_fractions[t]), ALL)
        first_product(1)
        for t in range(PACK):
            gather(x0[:, t, :], 0, t, ALL)

        w3_stage = (stage[3][:], stage[0][:], stage[1][:])

        def quantize_w3(a):
            return quantize(interleave(nc.scalar.copy, w3_stage[a], w3_raw[a][:]), PASS, "w3_%d" % a)

        w3_q = [quantize_w3(0)]
        wholes = [terms[:, 1, :]] + [lent(i, 1) for i in range(PACK - 1)]
        for t in range(PACK):
            scatter(1, t, sine(sines[t][:], fraction_by_transposes(t, w3_raw[0][:, t, :], wholes[t])), ALL)
        w3_q += [quantize_w3(a) for a in range(1, K_PASSES)]
        x0_q = quantize(interleave(nc.scalar.copy, stage[2][:], x0[:]), PASS, "x0")

        def w4_pass(c, b, x_operand):
            for n in range(N_TILES):
                weights = w4_t[:, b, 2 * P * n : 2 * P * (n + 1)].bitcast(FP4X4), w4_plane[:, b, block(n)]
                closes = b == H_PASSES - 1 and n == N_TILES - 1
                multiply(turned[c][:, block(n)], weights, x_operand, False, closes)

        for a in range(K_PASSES):
            for c in range(CHUNKS):
                for n in range(N_TILES):
                    opens = a == 0 and n == 0
                    multiply(turned[c][:, block(n)], columns(w3_q[a], block(n)), v_operand(a, block(c)), opens, False)
        for c in range(CHUNKS):
            w4_pass(c, 0, columns(x0_q, block(c)))

        x1_bytes = (sines[PACK - 1][:], wgs_gain[1, PACK - 1])
        x1_rounded = [stage[c][:, 2 * S : 3 * S] for c in range(CHUNKS)]

        def finish_chunk(c):
            w4_pass(c, 1, columns(quantize(x1_rounded[c], P, "x1_%d" % c), slice(0, P)))

        for c in range(CHUNKS):
            x1 = x1_bytes[c % 2].rearrange("k (t m) -> k t m", t=PACK)
            for t in range(PACK):
                gather(x1[:, t, :], 1, t, block(c))
            if c > 0:
                finish_chunk(c - 1)
            interleave(nc.vector.tensor_copy if c == CHUNKS - 1 else nc.scalar.copy, x1_rounded[c], x1)
        finish_chunk(CHUNKS - 1)

        out_view = out.rearrange("(n p) m -> p n m", p=P)
        for c in range(CHUNKS):
            result = ring.tile([P, N_TILES, P], F32, name="result", tag="raw", bufs=RAW_BUFS)
            for n in range(N_TILES):
                nc.scalar.activation(
                    out=result[:, n, :], in_=turned[c][:, block(n)], func=ACT.Tanh, bias=bias_t[:, n : n + 1]
                )
            parts = 2 if c == CHUNKS - 1 else 1
            for part in range(parts):
                tiles = slice(part * N_TILES // parts, (part + 1) * N_TILES // parts)
                nc.sync.dma_start(out=out_view[:, tiles, block(c)], in_=result[:, tiles, :])
